import numpy as np
import ml_dtypes


def mxq(x, axis, fmt="e4m3"):
    dtype, down = {"e4m3": (ml_dtypes.float8_e4m3fn, 7), "e5m2": (ml_dtypes.float8_e5m2, 14)}[fmt]
    v = np.moveaxis(np.asarray(x, np.float32).astype(ml_dtypes.bfloat16).astype(np.float64), axis, -1)
    blocks = v.reshape(v.shape[:-1] + (-1, 32))
    amax = np.abs(blocks).max(-1, keepdims=True)
    byte = np.maximum(np.where(amax > 0, np.frexp(amax)[1] - 1 + 127, 0) - down, 1)
    scale = np.exp2(byte - 127.0)
    codes = (blocks / scale).astype(np.float32).astype(dtype).astype(np.float64)
    return np.moveaxis((codes * scale).reshape(v.shape), -1, axis)


WIDE = False


def mx_kscale(k):
    if not WIDE:
        return np.ones(k)
    levels = np.array([24, -24, 12, -12, 0])
    if k % 512:
        return np.exp2(np.random.permutation(np.resize(levels, k // 32))).repeat(32)
    a = np.empty((k // 512, 16))
    for p in range(k // 512):
        a[p, :8] = np.random.permutation(np.resize(levels, 8))
        for g in range(8):
            far = levels[np.abs(levels - a[p, g]) >= 10]
            a[p, g + 8] = far[np.random.randint(len(far))]
    return np.exp2(a.ravel()).repeat(32)


def f64(x):
    return np.asarray(x).astype(np.float64)


def striped(idx):
    return np.tile(idx.reshape(-1, 16).T, (8, 1)).astype(np.uint16)


def unstriped(offs):
    return offs[:16].T.reshape(-1).astype(np.int64)


def striped8(idx):
    return np.concatenate([v.reshape(-1, 16).T for v in idx]).astype(np.uint16)


def unstriped8(offs):
    return np.stack([offs[16 * g:16 * g + 16].T.reshape(-1) for g in range(8)]).astype(np.int64)


E2M1 = np.array([0.0, 0.5, 1.0, 1.5, 2.0, 3.0, 4.0, 6.0, -0.0, -0.5, -1.0, -1.5, -2.0, -3.0, -4.0, -6.0])


def pack_weight(w, fmt):
    k, n = w.shape
    w = f64(np.asarray(w, np.float32).astype(ml_dtypes.bfloat16)).reshape(k // 32, 32, n)
    amax = np.abs(w).max(1)
    if fmt == "e4m3":
        byte = np.frexp(amax)[1] - 1 + 127 - 7
    else:
        mant, ex = np.frexp(amax / 6.0)
        byte = np.where(mant > 0.5, ex, ex - 1) + 127
    byte = np.clip(np.where(amax > 0, byte, 1), 1, 254)
    scaled = (w * np.exp2(127.0 - byte)[:, None, :]).reshape(k, n).astype(np.float32)
    by_word = np.ascontiguousarray(scaled.reshape(k // 512, 128, 4, n).transpose(0, 1, 3, 2))
    if fmt == "e4m3":
        words = by_word.astype(ml_dtypes.float8_e4m3fn).view(np.uint8)
    else:
        c = by_word.astype(ml_dtypes.float4_e2m1fn).view(np.uint8) & 0xF
        words = (c[..., 0::2] | (c[..., 1::2] << 4)).reshape(k // 512, 128, 2 * n)
    return np.ascontiguousarray(words), np.ascontiguousarray(byte.astype(np.uint8).reshape(k // 512, 16, n))


def unpack_weight(words, scales, fmt):
    g, _, n = scales.shape
    words = np.ascontiguousarray(words).reshape(g, 128, n, -1)
    if fmt == "e4m3":
        vals = words.view(ml_dtypes.float8_e4m3fn).astype(np.float64)
    else:
        nib = np.empty((g, 128, n, 4), np.uint8)
        nib[..., 0::2] = words & 0xF
        nib[..., 1::2] = words >> 4
        vals = E2M1[nib]
    vals = vals * np.repeat(np.exp2(scales.astype(np.float64) - 127.0), 8, axis=1)[..., None]
    return vals.transpose(0, 1, 3, 2).reshape(g * 512, n)


def pack_table4(v):
    words, scales = pack_weight(v, "e2m1")
    g, t = words.shape[0] // 2, v.shape[1]
    return np.ascontiguousarray(words.reshape(g, 2, 128, t, 2).transpose(0, 2, 3, 1, 4).reshape(g, 128, t, 4)), scales


def unpack_table4(words, scales):
    g, _, t, _ = words.shape
    return unpack_weight(words.reshape(g, 128, t, 2, 2).transpose(0, 3, 1, 2, 4).reshape(2 * g, 128, 2 * t), scales, "e2m1")


K, L, R, N, T, J = 512, 1024, 512, 512, 2048, 1024


def setup_inputs():
    n = np.random.standard_normal
    s = mx_kscale(K)[:, None]
    s2 = mx_kscale(L)[:, None]
    u = mx_kscale(R)[:, None]
    p_tab = pack_table4(n((L, T)) * s2)
    p_wa = pack_weight(n((K, R)) / np.sqrt(K) / s * u.T, "e2m1")
    p_wb = pack_weight(n((L, R)) / np.sqrt(L) / s2, "e2m1")
    return {
        "tab_words": p_tab[0],
        "tab_scales": p_tab[1],
        "xT": (n((K, T)) * s).astype(np.float32),
        "wgt2": np.repeat(np.random.uniform(0.5, 2.0, (8, J)), 16, axis=0).astype(np.float32),
        "wa_words": p_wa[0],
        "wa_scales": p_wa[1],
        "wb_words": p_wb[0],
        "wb_scales": p_wb[1],
        "wd": (n((R, N)) / np.sqrt(R) / u).astype(np.float32),
        "res": (n((N, J))).astype(np.float32),
        "offs": striped(np.random.permutation(T)[:J]),
        "offs2": striped8(np.stack([np.random.permutation(T)[:J] for _ in range(8)])),
    }


def reference(tab_words, tab_scales, xT, wgt2, wa_words, wa_scales, wb_words, wb_scales, wd, res, offs, offs2):
    idx = unstriped(offs)
    idx2 = unstriped8(offs2)
    tab_ = unpack_table4(tab_words, tab_scales)[:, idx]
    rows = np.arange(K)
    xg = f64(wgt2)[rows // 4 % 128] * f64(xT)[rows[:, None], idx2[rows % 512 // 64]]
    xT_ = mxq(xg, 0, "e4m3")
    wa_ = unpack_weight(wa_words, wa_scales, "e2m1")
    wb_ = unpack_weight(wb_words, wb_scales, "e2m1")
    ya = wa_.T @ xT_
    yb = wb_.T @ tab_
    h = ya * yb
    h_ = mxq(h, 0, "e4m3")
    wd_ = mxq(f64(wd), 0, "e4m3")
    y = wd_.T @ h_
    return f64(res) + y

@@ -1,0 +1,245 @@
+from contextlib import ExitStack
+
+import concourse.mybir as mybir
+
+K, L, R, N, T, J = 512, 1024, 512, 512, 2048, 1024
+FLOPS = 2 * J * R * (K + L + N)
+
+F32 = mybir.dt.float32
+BF16 = mybir.dt.bfloat16
+I32 = mybir.dt.int32
+U32 = mybir.dt.uint32
+U16 = mybir.dt.uint16
+U8 = mybir.dt.uint8
+FP8X4 = mybir.dt.float8_e4m3fn_x4
+FP4X4 = mybir.dt.float4_e2m1fn_x4
+MULT = mybir.AluOpType.mult
+ADD = mybir.AluOpType.add
+
+P = 128
+PACK = 4
+GROUP = 128
+HALF = J // 2
+CHUNKS = (256, 256, 256, 256)
+BANK = 512
+
+
+def tile_list_htabg_mul_res_kernel(
+    tc, tab_words, tab_scales, xT, wgt2, wa_words, wa_scales, wb_words, wb_scales, wd, res, offs, offs2, out
+):
+    nc = tc.nc
+    with ExitStack() as ctx:
+        keep = ctx.enter_context(tc.tile_pool(name="keep", bufs=1))
+        psum = ctx.enter_context(tc.psum_pool(name="psum", bufs=4))
+
+        def sb(name, shape, dtype):
+            return keep.tile(shape, dtype, name=name, align_bytes=64)
+
+        idx = sb("idx", [P, J // 16], U16)
+        idx2 = sb("idx2", [P, J // 16], U16)
+        tab_w = sb("tab_w", [P, T], I32)
+        tab_s = sb("tab_s", [P, T // 4], I32)
+        wgt = sb("wgt", [P, J], F32)
+        x_planes = [sb("x_plane%d" % i, [P, T], F32) for i in range(PACK)]
+        wa_w_raw = sb("wa_w_raw", [P, 256], I32)
+        wa_s_raw = sb("wa_s_raw", [P, 128], I32)
+        wb_w_raw = sb("wb_w_raw", [P, 2, 256], I32)
+        wb_s_raw = sb("wb_s_raw", [P, 2, 128], I32)
+        wa_w = sb("wa_w", [P, PACK, 64], I32)
+        wa_s = sb("wa_s", [P, PACK, 32], I32)
+        wb_w = sb("wb_w", [P, PACK, 2, 64], I32)
+        wb_s = sb("wb_s", [P, PACK, 2, 32], I32)
+        wd_raw = sb("wd_raw", [P, PACK, N], F32)
+        res_sb = sb("res_sb", [P, N // P, J], F32)
+        v_pairs = sb("v_pairs", [P, J], U32)
+        v_w = sb("v_w", [P, 2, 2, 2 * HALF], U8)
+        v_s0 = sb("v_s0", [P, J], U8)
+        v_s1 = sb("v_s1", [P, J // 4], I32)
+        yb = sb("yb", [P, J, PACK], F32)
+        xg = sb("xg", [P, PACK, J], F32)
+        xb = sb("xb", [P, J, PACK], BF16)
+        x_codes = sb("x_codes", [P, J], U32)
+        x_scales = sb("x_scales", [P, J], U8)
+        wd_b = sb("wd_b", [P, N, PACK], BF16)
+        wd_codes = sb("wd_codes", [P, N], U32)
+        wd_scales = sb("wd_scales", [P, N], U8)
+        hb = sb("hb", [P, J, PACK], BF16)
+        h_codes = sb("h_codes", [P, J], U32)
+        h_scales = sb("h_scales", [P, J], U8)
+        out_sb = sb("out_sb", [P, N // P, J], F32)
+
+        nc.vector.memset(tab_s[:], 0)
+        nc.vector.memset(wb_s_raw[:], 0)
+        nc.vector.memset(wa_s_raw[:], 0)
+        nc.vector.memset(v_s1[:], 0)
+
+        x_rows = xT.rearrange("(p i) t -> i p t", i=PACK)
+        wd_rows = wd.rearrange("(g t q) n -> t g q n", t=PACK, q=8)
+        res_rows = res.rearrange("(b p) j -> p b j", p=P)
+        out_rows = out.rearrange("(b p) j -> p b j", p=P)
+
+        nc.sync.dma_start(idx[:], offs)
+        for q in range(4):
+            nc.sync.dma_start(tab_s[32 * q : 32 * q + 8, :], tab_scales[:, 4 * q : 4 * q + 4, :].bitcast(I32))
+        nc.sync.dma_start(wb_w_raw[:], wb_words.rearrange("a p c -> p a c").bitcast(I32))
+        nc.sync.dma_start(tab_w[:], tab_words[0].rearrange("p t b -> p (t b)").bitcast(I32))
+        for q in range(4):
+            nc.sync.dma_start(
+                wb_s_raw[32 * q : 32 * q + 4], wb_scales[:, 4 * q : 4 * q + 4, :].rearrange("a q c -> q a c").bitcast(I32)
+            )
+        nc.sync.dma_start(idx2[:], offs2)
+        nc.sync.dma_start(wgt[:], wgt2)
+        nc.sync.dma_start(x_planes[0][:], x_rows[0])
+        nc.sync.dma_start(x_planes[1][:], x_rows[1])
+        nc.sync.dma_start(wa_w_raw[:], wa_words[0].bitcast(I32))
+        for q in range(4):
+            nc.sync.dma_start(wa_s_raw[32 * q : 32 * q + 4, :], wa_scales[0, 4 * q : 4 * q + 4, :].bitcast(I32))
+        nc.sync.dma_start(x_planes[2][:], x_rows[2])
+        nc.sync.dma_start(x_planes[3][:], x_rows[3])
+        for t in range(PACK):
+            nc.sync.dma_start(wd_raw[:, t, :], wd_rows[t])
+        for half in range(2):
+            cols = slice(half * HALF, (half + 1) * HALF)
+            nc.sync.dma_start(res_sb[:, :, cols], res_rows[:, :, cols])
+
+        def entries(cols):
+            return slice(cols.start // 16, cols.stop // 16)
+
+        nc.vector.tensor_copy(v_s0[:], tab_s[:].bitcast(U8).indirect(idx[:]))
+        nc.scalar.dma_start(v_s1[0:112, :], v_s0[4:116, :].bitcast(I32))
+        nc.vector.tensor_copy(
+            wb_w[:].rearrange("p t a (g e) -> p t (a g) e", e=4), wb_w_raw[:].rearrange("p a (g t e) -> p t (a g) e", t=PACK, e=4)
+        )
+        for half in range(2):
+            cols = slice(half * HALF, (half + 1) * HALF)
+            nc.vector.tensor_copy(v_pairs[:, cols], tab_w[:].bitcast(U32).indirect(idx[:, entries(cols)]))
+        nc.vector.tensor_copy(
+            wb_s[:].rearrange("p t a (g e) -> p t (a g) e", e=2), wb_s_raw[:].rearrange("p a (g t e) -> p t (a g) e", t=PACK, e=2)
+        )
+        for half in range(2):
+            cols = slice(half * HALF, (half + 1) * HALF)
+            nc.vector.tensor_copy(
+                v_w[:, half].bitcast(U16), v_pairs[:, cols].bitcast(U16).rearrange("p (j a) -> p a j", a=2)
+            )
+        v_scales = (v_s0[:], v_s1[:].bitcast(U8))
+
+        for j0 in range(0, J, GROUP):
+            cols = slice(j0, j0 + GROUP)
+            half, within = divmod(j0, HALF)
+            bank = psum.tile([P, PACK, GROUP], F32, name="first")
+            for t in range(PACK):
+                for a in range(2):
+                    nc.tensor.matmul_mx(
+                        out=bank[:, t, :],
+                        lhsT=wb_w[:, t, a, :].bitcast(FP4X4),
+                        lhsT_scale=wb_s[:, t, a, :].bitcast(U8),
+                        rhs=v_w[:, half, a, 2 * within : 2 * (within + GROUP)].bitcast(FP4X4),
+                        rhs_scale=v_scales[a][:, cols],
+                        start=(a == 0),
+                        stop=(a == 1),
+                    )
+            nc.scalar.copy(yb[:, cols, :], bank[:].rearrange("p t j -> p j t"))
+
+        def gather_x(i, cols):
+            nc.vector.tensor_tensor(xg[:, i, cols], x_planes[i][:].indirect(idx2[:, entries(cols)]), wgt[:, cols], MULT)
+
+        def round_pair(i, cols):
+            nc.scalar.copy(xb[:, cols, i : i + 2], xg[:, i : i + 2, cols].rearrange("p i j -> p j i"))
+
+        for i in range(PACK - 1):
+            for half in range(2):
+                cols = slice(half * HALF, (half + 1) * HALF)
+                gather_x(i, cols)
+                if i == 1:
+                    round_pair(0, cols)
+            if i == 1:
+                nc.vector.tensor_copy(
+                    wa_w[:].rearrange("p t (g e) -> p t g e", e=4), wa_w_raw[:].rearrange("p (g t e) -> p t g e", t=PACK, e=4)
+                )
+                nc.vector.tensor_copy(
+                    wa_s[:].rearrange("p t (g e) -> p t g e", e=2), wa_s_raw[:].rearrange("p (g t e) -> p t g e", t=PACK, e=2)
+                )
+
+        def quantize(codes, scales, values, cols):
+            nc.vector.quantize_mx(
+                out=codes[:, cols].bitcast(FP8X4), scales=scales[:, cols], in_=values[:, cols, :].rearrange("p j t -> p (j t)")
+            )
+
+        starts = [sum(CHUNKS[:c]) for c in range(len(CHUNKS))]
+        spans = [slice(s, s + w) for s, w in zip(starts, CHUNKS)]
+
+        def last_plane(c):
+            gather_x(PACK - 1, spans[c])
+            round_pair(2, spans[c])
+
+        def product(c):
+            for j0 in range(spans[c].start, spans[c].stop, GROUP):
+                group = slice(j0, j0 + GROUP)
+                bank = psum.tile([P, PACK, GROUP], F32, name="first")
+                for t in range(PACK):
+                    nc.tensor.matmul_mx(
+                        out=bank[:, t, :],
+                        lhsT=wa_w[:, t, :].bitcast(FP4X4),
+                        lhsT_scale=wa_s[:, t, :].bitcast(U8),
+                        rhs=x_codes[:, group].bitcast(FP8X4),
+                        rhs_scale=x_scales[:, group],
+                        start=True,
+                        stop=True,
+                    )
+                nc.vector.tensor_tensor(hb[:, group, :], bank[:].rearrange("p t j -> p j t"), yb[:, group, :], MULT)
+
+        def finish(c, b0):
+            cols = spans[c]
+            bank = psum.tile([P, 2, cols.stop - cols.start], F32, name="second")
+            for b in range(2):
+                n_cols = slice((b0 + b) * P, (b0 + b + 1) * P)
+                nc.tensor.matmul_mx(
+                    out=bank[:, b, :],
+                    lhsT=wd_codes[:, n_cols].bitcast(FP8X4),
+                    lhsT_scale=wd_scales[:, n_cols],
+                    rhs=h_codes[:, cols].bitcast(FP8X4),
+                    rhs_scale=h_scales[:, cols],
+                    start=True,
+                    stop=True,
+                )
+            blocks = slice(b0, b0 + 2)
+            nc.vector.tensor_tensor(out_sb[:, blocks, cols], bank[:], res_sb[:, blocks, cols], ADD)
+            nc.sync.dma_start(out_rows[:, blocks, cols], out_sb[:, blocks, cols])
+
+        def wd_half(half):
+            n_cols = slice(half * N // 2, (half + 1) * N // 2)
+            nc.scalar.copy(wd_b[:, n_cols, :], wd_raw[:, :, n_cols].rearrange("p t n -> p n t"))
+            quantize(wd_codes, wd_scales, wd_b, n_cols)
+
+        def quantize_x(c):
+            quantize(x_codes, x_scales, xb, spans[c])
+
+        def quantize_h(c):
+            quantize(h_codes, h_scales, hb, spans[c])
+
+        last_plane(0)
+        last_plane(1)
+        last_plane(2)
+        quantize_x(0)
+        last_plane(3)
+        quantize_x(1)
+        product(0)
+        quantize_x(2)
+        quantize_h(0)
+        product(1)
+        quantize_x(3)
+        quantize_h(1)
+        wd_half(0)
+        wd_half(1)
+        finish(0, 0)
+        finish(0, 2)
+        product(2)
+        finish(1, 0)
+        quantize_h(2)
+        finish(1, 2)
+        product(3)
+        finish(2, 0)
+        quantize_h(3)
+        finish(2, 2)
+        finish(3, 0)
+        finish(3, 2)

@@ -90,6 +90,12 @@ def tile_list_htabg_mul_res_kernel(
         nc.sync.dma_start(idx2[:], offs2)
         nc.sync.dma_start(wgt[:], wgt2)
         nc.sync.dma_start(x_planes[0][:], x_rows[0])
+
+        def entries(cols):
+            return slice(cols.start // 16, cols.stop // 16)
+
+        nc.vector.tensor_copy(v_s0[:], tab_s[:].bitcast(U8).indirect(idx[:]))
+        nc.sync.dma_start(v_s1[0:112, :], v_s0[4:116, :].bitcast(I32))
         nc.sync.dma_start(x_planes[1][:], x_rows[1])
         nc.sync.dma_start(wa_w_raw[:], wa_words[0].bitcast(I32))
         for q in range(4):
@@ -102,11 +108,6 @@ def tile_list_htabg_mul_res_kernel(
             cols = slice(half * HALF, (half + 1) * HALF)
             nc.sync.dma_start(res_sb[:, :, cols], res_rows[:, :, cols])
 
-        def entries(cols):
-            return slice(cols.start // 16, cols.stop // 16)
-
-        nc.vector.tensor_copy(v_s0[:], tab_s[:].bitcast(U8).indirect(idx[:]))
-        nc.scalar.dma_start(v_s1[0:112, :], v_s0[4:116, :].bitcast(I32))
         nc.vector.tensor_copy(
             wb_w[:].rearrange("p t a (g e) -> p t (a g) e", e=4), wb_w_raw[:].rearrange("p a (g t e) -> p t (a g) e", t=PACK, e=4)
         )

@@ -66,6 +66,7 @@ def tile_list_htabg_mul_res_kernel(
         hb = sb("hb", [P, J, PACK], BF16)
         h_codes = sb("h_codes", [P, J], U32)
         h_scales = sb("h_scales", [P, J], U8)
+        y_sb = sb("y_sb", [P, 2, HALF], F32)
         out_sb = sb("out_sb", [P, N // P, J], F32)
 
         nc.vector.memset(tab_s[:], 0)
@@ -144,15 +145,15 @@ def tile_list_htabg_mul_res_kernel(
         def gather_x(i, cols):
             nc.vector.tensor_tensor(xg[:, i, cols], x_planes[i][:].indirect(idx2[:, entries(cols)]), wgt[:, cols], MULT)
 
-        def round_pair(i, cols):
-            nc.scalar.copy(xb[:, cols, i : i + 2], xg[:, i : i + 2, cols].rearrange("p i j -> p j i"))
+        def round_planes(first, stop, cols):
+            nc.scalar.copy(xb[:, cols, first:stop], xg[:, first:stop, cols].rearrange("p i j -> p j i"))
 
         for i in range(PACK - 1):
             for half in range(2):
                 cols = slice(half * HALF, (half + 1) * HALF)
                 gather_x(i, cols)
-                if i == 1:
-                    round_pair(0, cols)
+                if (i, half) == (1, 0):
+                    round_planes(0, 2, cols)
             if i == 1:
                 nc.vector.tensor_copy(
                     wa_w[:].rearrange("p t (g e) -> p t g e", e=4), wa_w_raw[:].rearrange("p (g t e) -> p t g e", t=PACK, e=4)
@@ -171,7 +172,7 @@ def tile_list_htabg_mul_res_kernel(
 
         def last_plane(c):
             gather_x(PACK - 1, spans[c])
-            round_pair(2, spans[c])
+            round_planes(2 if spans[c].stop <= HALF else 0, PACK, spans[c])
 
         def product(c):
             for j0 in range(spans[c].start, spans[c].stop, GROUP):
@@ -204,8 +205,14 @@ def tile_list_htabg_mul_res_kernel(
                     stop=True,
                 )
             blocks = slice(b0, b0 + 2)
-            nc.vector.tensor_tensor(out_sb[:, blocks, cols], bank[:], res_sb[:, blocks, cols], ADD)
-            nc.sync.dma_start(out_rows[:, blocks, cols], out_sb[:, blocks, cols])
+            if c < 2 and b0 == 0:
+                nc.scalar.copy(y_sb[:, :, cols], bank[:])
+                for b in range(2):
+                    nc.gpsimd.tensor_tensor(out_sb[:, b, cols], y_sb[:, b, cols], res_sb[:, b, cols], ADD)
+                nc.scalar.dma_start(out_rows[:, blocks, cols], out_sb[:, blocks, cols])
+            else:
+                nc.vector.tensor_tensor(out_sb[:, blocks, cols], bank[:], res_sb[:, blocks, cols], ADD)
+                nc.sync.dma_start(out_rows[:, blocks, cols], out_sb[:, blocks, cols])
 
         def wd_half(half):
             n_cols = slice(half * N // 2, (half + 1) * N // 2)
@@ -231,16 +238,16 @@ def tile_list_htabg_mul_res_kernel(
         quantize_x(3)
         quantize_h(1)
         wd_half(0)
-        wd_half(1)
         finish(0, 0)
-        finish(0, 2)
-        product(2)
         finish(1, 0)
+        product(2)
+        wd_half(1)
         quantize_h(2)
-        finish(1, 2)
+        finish(0, 2)
         product(3)
-        finish(2, 0)
+        finish(1, 2)
         quantize_h(3)
+        finish(2, 0)
         finish(2, 2)
         finish(3, 0)
         finish(3, 2)

@@ -32,8 +32,8 @@ def tile_list_htabg_mul_res_kernel(
         keep = ctx.enter_context(tc.tile_pool(name="keep", bufs=1))
         psum = ctx.enter_context(tc.psum_pool(name="psum", bufs=4))
 
-        def sb(name, shape, dtype):
-            return keep.tile(shape, dtype, name=name, align_bytes=64)
+        def sb(name, shape, dtype, on=""):
+            return keep.tile(shape, dtype, name=name, tag=on or name, align_bytes=64)
 
         idx = sb("idx", [P, J // 16], U16)
         idx2 = sb("idx2", [P, J // 16], U16)
@@ -63,10 +63,10 @@ def tile_list_htabg_mul_res_kernel(
         wd_b = sb("wd_b", [P, N, PACK], BF16)
         wd_codes = sb("wd_codes", [P, N], U32)
         wd_scales = sb("wd_scales", [P, N], U8)
-        hb = sb("hb", [P, J, PACK], BF16)
+        hb = [sb("hb%d" % c, [P, w, PACK], BF16) for c, w in enumerate(CHUNKS)]
         h_codes = sb("h_codes", [P, J], U32)
         h_scales = sb("h_scales", [P, J], U8)
-        y_sb = sb("y_sb", [P, 2, HALF], F32)
+        y_sb = sb("y_sb", [P, 2, 2, 256], F32)
         out_sb = sb("out_sb", [P, N // P, J], F32)
 
         nc.vector.memset(tab_s[:], 0)
@@ -79,28 +79,33 @@ def tile_list_htabg_mul_res_kernel(
         res_rows = res.rearrange("(b p) j -> p b j", p=P)
         out_rows = out.rearrange("(b p) j -> p b j", p=P)
 
+        def entries(cols):
+            return slice(cols.start // 16, cols.stop // 16)
+
+        def quantize(codes, scales, values, cols):
+            nc.vector.quantize_mx(
+                out=codes[:, cols].bitcast(FP8X4), scales=scales[:, cols], in_=values[:, cols, :].rearrange("p j t -> p (j t)")
+            )
+
         nc.sync.dma_start(idx[:], offs)
-        for q in range(4):
-            nc.sync.dma_start(tab_s[32 * q : 32 * q + 8, :], tab_scales[:, 4 * q : 4 * q + 4, :].bitcast(I32))
-        nc.sync.dma_start(wb_w_raw[:], wb_words.rearrange("a p c -> p a c").bitcast(I32))
+        nc.sync.dma_start(idx2[:], offs2)
+        tab_rows = tab_scales.rearrange("a (q s) t -> s q a t", s=4)
+        for s in range(4):
+            nc.sync.dma_start(tab_s[s:P:16, :], tab_rows[s].bitcast(I32))
         nc.sync.dma_start(tab_w[:], tab_words[0].rearrange("p t b -> p (t b)").bitcast(I32))
+        nc.sync.dma_start(wb_w_raw[:], wb_words.rearrange("a p c -> p a c").bitcast(I32))
+        nc.sync.dma_start(wgt[:], wgt2)
         for q in range(4):
             nc.sync.dma_start(
                 wb_s_raw[32 * q : 32 * q + 4], wb_scales[:, 4 * q : 4 * q + 4, :].rearrange("a q c -> q a c").bitcast(I32)
             )
-        nc.sync.dma_start(idx2[:], offs2)
-        nc.sync.dma_start(wgt[:], wgt2)
         nc.sync.dma_start(x_planes[0][:], x_rows[0])
-
-        def entries(cols):
-            return slice(cols.start // 16, cols.stop // 16)
-
         nc.vector.tensor_copy(v_s0[:], tab_s[:].bitcast(U8).indirect(idx[:]))
-        nc.sync.dma_start(v_s1[0:112, :], v_s0[4:116, :].bitcast(I32))
+        nc.sync.dma_start(v_s1[0:112, :], v_s0[16:128, :].bitcast(I32))
         nc.sync.dma_start(x_planes[1][:], x_rows[1])
-        nc.sync.dma_start(wa_w_raw[:], wa_words[0].bitcast(I32))
         for q in range(4):
             nc.sync.dma_start(wa_s_raw[32 * q : 32 * q + 4, :], wa_scales[0, 4 * q : 4 * q + 4, :].bitcast(I32))
+        nc.sync.dma_start(wa_w_raw[:], wa_words[0].bitcast(I32))
         nc.sync.dma_start(x_planes[2][:], x_rows[2])
         nc.sync.dma_start(x_planes[3][:], x_rows[3])
         for t in range(PACK):
@@ -109,12 +114,12 @@ def tile_list_htabg_mul_res_kernel(
             cols = slice(half * HALF, (half + 1) * HALF)
             nc.sync.dma_start(res_sb[:, :, cols], res_rows[:, :, cols])
 
-        nc.vector.tensor_copy(
-            wb_w[:].rearrange("p t a (g e) -> p t (a g) e", e=4), wb_w_raw[:].rearrange("p a (g t e) -> p t (a g) e", t=PACK, e=4)
-        )
         for half in range(2):
             cols = slice(half * HALF, (half + 1) * HALF)
             nc.vector.tensor_copy(v_pairs[:, cols], tab_w[:].bitcast(U32).indirect(idx[:, entries(cols)]))
+        nc.vector.tensor_copy(
+            wb_w[:].rearrange("p t a (g e) -> p t (a g) e", e=4), wb_w_raw[:].rearrange("p a (g t e) -> p t (a g) e", t=PACK, e=4)
+        )
         nc.vector.tensor_copy(
             wb_s[:].rearrange("p t a (g e) -> p t (a g) e", e=2), wb_s_raw[:].rearrange("p a (g t e) -> p t (a g) e", t=PACK, e=2)
         )
@@ -142,11 +147,14 @@ def tile_list_htabg_mul_res_kernel(
                     )
             nc.scalar.copy(yb[:, cols, :], bank[:].rearrange("p t j -> p j t"))
 
+        def interleave(packed, planes):
+            nc.scalar.copy(packed.rearrange("p (c e) t -> p c t e", e=4), planes.rearrange("p t (c e) -> p c t e", e=4))
+
         def gather_x(i, cols):
             nc.vector.tensor_tensor(xg[:, i, cols], x_planes[i][:].indirect(idx2[:, entries(cols)]), wgt[:, cols], MULT)
 
         def round_planes(first, stop, cols):
-            nc.scalar.copy(xb[:, cols, first:stop], xg[:, first:stop, cols].rearrange("p i j -> p j i"))
+            interleave(xb[:, cols, first:stop], xg[:, first:stop, cols])
 
         for i in range(PACK - 1):
             for half in range(2):
@@ -161,11 +169,6 @@ def tile_list_htabg_mul_res_kernel(
                 nc.vector.tensor_copy(
                     wa_s[:].rearrange("p t (g e) -> p t g e", e=2), wa_s_raw[:].rearrange("p (g t e) -> p t g e", t=PACK, e=2)
                 )
-
-        def quantize(codes, scales, values, cols):
-            nc.vector.quantize_mx(
-                out=codes[:, cols].bitcast(FP8X4), scales=scales[:, cols], in_=values[:, cols, :].rearrange("p j t -> p (j t)")
-            )
 
         starts = [sum(CHUNKS[:c]) for c in range(len(CHUNKS))]
         spans = [slice(s, s + w) for s, w in zip(starts, CHUNKS)]
@@ -188,9 +191,9 @@ def tile_list_htabg_mul_res_kernel(
                         start=True,
                         stop=True,
                     )
-                nc.vector.tensor_tensor(hb[:, group, :], bank[:].rearrange("p t j -> p j t"), yb[:, group, :], MULT)
+                nc.vector.tensor_tensor(hb[c][:, j0 - spans[c].start : j0 - spans[c].start + GROUP, :], bank[:].rearrange("p t j -> p j t"), yb[:, group, :], MULT)
 
-        def finish(c, b0):
+        def second(c, b0):
             cols = spans[c]
             bank = psum.tile([P, 2, cols.stop - cols.start], F32, name="second")
             for b in range(2):
@@ -204,26 +207,33 @@ def tile_list_htabg_mul_res_kernel(
                     start=True,
                     stop=True,
                 )
-            blocks = slice(b0, b0 + 2)
-            if c < 2 and b0 == 0:
-                nc.scalar.copy(y_sb[:, :, cols], bank[:])
-                for b in range(2):
-                    nc.gpsimd.tensor_tensor(out_sb[:, b, cols], y_sb[:, b, cols], res_sb[:, b, cols], ADD)
-                nc.scalar.dma_start(out_rows[:, blocks, cols], out_sb[:, blocks, cols])
-            else:
-                nc.vector.tensor_tensor(out_sb[:, blocks, cols], bank[:], res_sb[:, blocks, cols], ADD)
-                nc.sync.dma_start(out_rows[:, blocks, cols], out_sb[:, blocks, cols])
+            return bank
+
+        def finish(c, b0):
+            cols, blocks = spans[c], slice(b0, b0 + 2)
+            nc.vector.tensor_tensor(out_sb[:, blocks, cols], second(c, b0)[:], res_sb[:, blocks, cols], ADD)
+            nc.sync.dma_start(out_rows[:, blocks, cols], out_sb[:, blocks, cols])
+
+        def copy_out(c, b0, k):
+            nc.scalar.copy(y_sb[:, k], second(c, b0)[:])
+
+        def finish_on_gpsimd(c, b0, k, sums):
+            for b in range(2):
+                nc.gpsimd.tensor_tensor(sums[:, b, :], y_sb[:, k, b, :], res_sb[:, b0 + b, spans[c]], ADD)
+            nc.scalar.dma_start(out_rows[:, b0 : b0 + 2, spans[c]], sums)
 
         def wd_half(half):
             n_cols = slice(half * N // 2, (half + 1) * N // 2)
-            nc.scalar.copy(wd_b[:, n_cols, :], wd_raw[:, :, n_cols].rearrange("p t n -> p n t"))
+            interleave(wd_b[:, n_cols, :], wd_raw[:, :, n_cols])
             quantize(wd_codes, wd_scales, wd_b, n_cols)
 
         def quantize_x(c):
             quantize(x_codes, x_scales, xb, spans[c])
 
         def quantize_h(c):
-            quantize(h_codes, h_scales, hb, spans[c])
+            nc.vector.quantize_mx(
+                out=h_codes[:, spans[c]].bitcast(FP8X4), scales=h_scales[:, spans[c]], in_=hb[c][:].rearrange("p j t -> p (j t)")
+            )
 
         last_plane(0)
         last_plane(1)
@@ -238,16 +248,22 @@ def tile_list_htabg_mul_res_kernel(
         quantize_x(3)
         quantize_h(1)
         wd_half(0)
-        finish(0, 0)
-        finish(1, 0)
         product(2)
         wd_half(1)
+        copy_out(0, 0, 0)
         quantize_h(2)
-        finish(0, 2)
+        finish(1, 0)
+        copy_out(0, 2, 1)
+        sums0 = sb("sums0", [P, 4, 256], F32, on="hb2")
+        finish_on_gpsimd(0, 0, 0, sums0[:, 0:2, :])
         product(3)
         finish(1, 2)
-        quantize_h(3)
+        finish_on_gpsimd(0, 2, 1, sums0[:, 2:4, :])
         finish(2, 0)
+        quantize_h(3)
         finish(2, 2)
         finish(3, 0)
-        finish(3, 2)
+        last = second(3, 2)
+        for b in range(2):
+            nc.vector.tensor_tensor(out_sb[:, 2 + b, spans[3]], last[:, b, :], res_sb[:, 2 + b, spans[3]], ADD)
+            (nc.sync, nc.scalar)[b].dma_start(out_rows[:, 2 + b, spans[3]], out_sb[:, 2 + b, spans[3]])

@@ -1,6 +1,7 @@
 from contextlib import ExitStack
 
 import concourse.mybir as mybir
+from concourse.masks import make_identity
 
 K, L, R, N, T, J = 512, 1024, 512, 512, 2048, 1024
 FLOPS = 2 * J * R * (K + L + N)
@@ -40,6 +41,9 @@ def tile_list_htabg_mul_res_kernel(
         tab_w = sb("tab_w", [P, T], I32)
         tab_s = sb("tab_s", [P, T // 4], I32)
         wgt = sb("wgt", [P, J], F32)
+        wgt_rows = sb("wgt_rows", [P, P], F32)
+        wgt_wide = sb("wgt_wide", [P, J], F32)
+        identity = sb("identity", [P, P], F32)
         x_planes = [sb("x_plane%d" % i, [P, T], F32) for i in range(PACK)]
         wa_w_raw = sb("wa_w_raw", [P, 256], I32)
         wa_s_raw = sb("wa_s_raw", [P, 128], I32)
@@ -73,6 +77,9 @@ def tile_list_htabg_mul_res_kernel(
         nc.vector.memset(wb_s_raw[:], 0)
         nc.vector.memset(wa_s_raw[:], 0)
         nc.vector.memset(v_s1[:], 0)
+        nc.vector.memset(wgt_rows[64:P, :], 0.0)
+        nc.vector.memset(identity[:], 0.0)
+        make_identity(nc, identity[:], nomemset=True)
 
         x_rows = xT.rearrange("(p i) t -> i p t", i=PACK)
         wd_rows = wd.rearrange("(g t q) n -> t g q n", t=PACK, q=8)
@@ -88,17 +95,17 @@ def tile_list_htabg_mul_res_kernel(
             )
 
         nc.sync.dma_start(idx[:], offs)
-        nc.sync.dma_start(idx2[:], offs2)
+        nc.sync.dma_start(wgt_rows[0:64, :], wgt2.rearrange("(g s) (b c) -> s b g c", s=16, c=P)[0])
         tab_rows = tab_scales.rearrange("a (q s) t -> s q a t", s=4)
         for s in range(4):
             nc.sync.dma_start(tab_s[s:P:16, :], tab_rows[s].bitcast(I32))
         nc.sync.dma_start(tab_w[:], tab_words[0].rearrange("p t b -> p (t b)").bitcast(I32))
         nc.sync.dma_start(wb_w_raw[:], wb_words.rearrange("a p c -> p a c").bitcast(I32))
-        nc.sync.dma_start(wgt[:], wgt2)
         for q in range(4):
             nc.sync.dma_start(
                 wb_s_raw[32 * q : 32 * q + 4], wb_scales[:, 4 * q : 4 * q + 4, :].rearrange("a q c -> q a c").bitcast(I32)
             )
+        nc.sync.dma_start(idx2[:], offs2)
         nc.sync.dma_start(x_planes[0][:], x_rows[0])
         nc.vector.tensor_copy(v_s0[:], tab_s[:].bitcast(U8).indirect(idx[:]))
         nc.sync.dma_start(v_s1[0:112, :], v_s0[16:128, :].bitcast(I32))
@@ -129,6 +136,17 @@ def tile_list_htabg_mul_res_kernel(
                 v_w[:, half].bitcast(U16), v_pairs[:, cols].bitcast(U16).rearrange("p (j a) -> p a j", a=2)
             )
         v_scales = (v_s0[:], v_s1[:].bitcast(U8))
+
+        turned = psum.tile([P, P], F32, name="second")
+        nc.tensor.transpose(turned[:], wgt_rows[:], identity[:])
+        nc.scalar.copy(
+            wgt_wide[:].rearrange("p (m s) -> p m s", s=16), turned[:, 0:64].unsqueeze(2).to_broadcast([P, 64, 16])
+        )
+        for j0 in range(0, J, 2 * P):
+            bank = psum.tile([P, 2 * P], F32, name="first")
+            for b in range(0, 2 * P, P):
+                nc.tensor.transpose(bank[:, b : b + P], wgt_wide[:, j0 + b : j0 + b + P], identity[:])
+            nc.scalar.copy(wgt[:, j0 : j0 + 2 * P], bank[:])
 
         for j0 in range(0, J, GROUP):
             cols = slice(j0, j0 + GROUP)

@@ -59,11 +59,9 @@ def tile_list_htabg_mul_res_kernel(
         v_w = sb("v_w", [P, 2, 2, 2 * HALF], U8)
         v_s0 = sb("v_s0", [P, J], U8)
         v_s1 = sb("v_s1", [P, J // 4], I32)
-        yb = sb("yb", [P, J, PACK], F32)
+        yb = [sb("yb%d" % g, [P, GROUP, PACK], F32) for g in range(J // GROUP)]
         xg = sb("xg", [P, PACK, J], F32)
-        xb = sb("xb", [P, J, PACK], BF16)
-        x_codes = sb("x_codes", [P, J], U32)
-        x_scales = sb("x_scales", [P, J], U8)
+        xb = [sb("xb%d" % c, [P, w, PACK], BF16) for c, w in enumerate(CHUNKS[:-1])]
         wd_b = sb("wd_b", [P, N, PACK], BF16)
         wd_codes = sb("wd_codes", [P, N], U32)
         wd_scales = sb("wd_scales", [P, N], U8)
@@ -108,7 +106,8 @@ def tile_list_htabg_mul_res_kernel(
         nc.sync.dma_start(idx2[:], offs2)
         nc.sync.dma_start(x_planes[0][:], x_rows[0])
         nc.vector.tensor_copy(v_s0[:], tab_s[:].bitcast(U8).indirect(idx[:]))
-        nc.sync.dma_start(v_s1[0:112, :], v_s0[16:128, :].bitcast(I32))
+        for q in range(0, P, 32):
+            nc.sync.dma_start(v_s1[q : q + 4, :], v_s0[q + 16 : q + 20, :].bitcast(I32))
         nc.sync.dma_start(x_planes[1][:], x_rows[1])
         for q in range(4):
             nc.sync.dma_start(wa_s_raw[32 * q : 32 * q + 4, :], wa_scales[0, 4 * q : 4 * q + 4, :].bitcast(I32))
@@ -163,23 +162,25 @@ def tile_list_htabg_mul_res_kernel(
                         start=(a == 0),
                         stop=(a == 1),
                     )
-            nc.scalar.copy(yb[:, cols, :], bank[:].rearrange("p t j -> p j t"))
+            nc.scalar.copy(yb[j0 // GROUP][:], bank[:].rearrange("p t j -> p j t"))
 
         def interleave(packed, planes):
             nc.scalar.copy(packed.rearrange("p (c e) t -> p c t e", e=4), planes.rearrange("p t (c e) -> p c t e", e=4))
 
-        def gather_x(i, cols):
-            nc.vector.tensor_tensor(xg[:, i, cols], x_planes[i][:].indirect(idx2[:, entries(cols)]), wgt[:, cols], MULT)
+        starts = [sum(CHUNKS[:c]) for c in range(len(CHUNKS))]
+        spans = [slice(s, s + w) for s, w in zip(starts, CHUNKS)]
 
-        def round_planes(first, stop, cols):
-            interleave(xb[:, cols, first:stop], xg[:, first:stop, cols])
+        def gather_x(i, cols, picked):
+            nc.vector.tensor_tensor(picked, x_planes[i][:].indirect(idx2[:, entries(cols)]), wgt[:, cols], MULT)
 
-        for i in range(PACK - 1):
-            for half in range(2):
-                cols = slice(half * HALF, (half + 1) * HALF)
-                gather_x(i, cols)
-                if (i, half) == (1, 0):
-                    round_planes(0, 2, cols)
+        def round_planes(first, stop, c):
+            interleave(xb[c][:, :, first:stop], xg[:, first:stop, spans[c]])
+
+        xg_first = sb("xg_first", [P, PACK, CHUNKS[0]], F32)
+        rest = slice(spans[1].start, J)
+        for i in range(2):
+            gather_x(i, spans[0], xg_first[:, i, :])
+            gather_x(i, rest, xg[:, i, rest])
             if i == 1:
                 nc.vector.tensor_copy(
                     wa_w[:].rearrange("p t (g e) -> p t g e", e=4), wa_w_raw[:].rearrange("p (g t e) -> p t g e", t=PACK, e=4)
@@ -188,28 +189,29 @@ def tile_list_htabg_mul_res_kernel(
                     wa_s[:].rearrange("p t (g e) -> p t g e", e=2), wa_s_raw[:].rearrange("p (g t e) -> p t g e", t=PACK, e=2)
                 )
 
-        starts = [sum(CHUNKS[:c]) for c in range(len(CHUNKS))]
-        spans = [slice(s, s + w) for s, w in zip(starts, CHUNKS)]
+        middle = slice(spans[1].start, spans[2].stop)
+        gather_x(2, spans[0], xg_first[:, 2, :])
+        gather_x(2, middle, xg[:, 2, middle])
 
         def last_plane(c):
-            gather_x(PACK - 1, spans[c])
-            round_planes(2 if spans[c].stop <= HALF else 0, PACK, spans[c])
+            gather_x(PACK - 1, spans[c], xg[:, PACK - 1, spans[c]])
+            round_planes(0, PACK, c)
 
         def product(c):
-            for j0 in range(spans[c].start, spans[c].stop, GROUP):
-                group = slice(j0, j0 + GROUP)
+            for j0 in range(0, CHUNKS[c], GROUP):
+                within = slice(j0, j0 + GROUP)
                 bank = psum.tile([P, PACK, GROUP], F32, name="first")
                 for t in range(PACK):
                     nc.tensor.matmul_mx(
                         out=bank[:, t, :],
                         lhsT=wa_w[:, t, :].bitcast(FP4X4),
                         lhsT_scale=wa_s[:, t, :].bitcast(U8),
-                        rhs=x_codes[:, group].bitcast(FP8X4),
-                        rhs_scale=x_scales[:, group],
+                        rhs=x_codes[c][:, within].bitcast(FP8X4),
+                        rhs_scale=x_scales[c][:, within],
                         start=True,
                         stop=True,
                     )
-                nc.vector.tensor_tensor(hb[c][:, j0 - spans[c].start : j0 - spans[c].start + GROUP, :], bank[:].rearrange("p t j -> p j t"), yb[:, group, :], MULT)
+                nc.vector.tensor_tensor(hb[c][:, within, :], bank[:].rearrange("p t j -> p j t"), yb[(spans[c].start + j0) // GROUP][:], MULT)
 
         def second(c, b0):
             cols = spans[c]
@@ -245,25 +247,36 @@ def tile_list_htabg_mul_res_kernel(
             interleave(wd_b[:, n_cols, :], wd_raw[:, :, n_cols])
             quantize(wd_codes, wd_scales, wd_b, n_cols)
 
-        def quantize_x(c):
-            quantize(x_codes, x_scales, xb, spans[c])
+        x_codes, x_scales = [], []
+
+        def quantize_x(c, on=""):
+            packed = sb("x_packed%d" % c, [P, CHUNKS[c] + CHUNKS[c] // 4], I32, on=on)
+            x_codes.append(packed[:, 0 : CHUNKS[c]])
+            x_scales.append(packed[:, CHUNKS[c] :].bitcast(U8))
+            nc.vector.quantize_mx(out=x_codes[c].bitcast(FP8X4), scales=x_scales[c], in_=xb[c][:].rearrange("p j t -> p (j t)"))
 
         def quantize_h(c):
             nc.vector.quantize_mx(
                 out=h_codes[:, spans[c]].bitcast(FP8X4), scales=h_scales[:, spans[c]], in_=hb[c][:].rearrange("p j t -> p (j t)")
             )
 
-        last_plane(0)
+        gather_x(PACK - 1, spans[0], xg_first[:, PACK - 1, :])
+        interleave(xb[0][:], xg_first[:])
         last_plane(1)
         last_plane(2)
         quantize_x(0)
-        last_plane(3)
+        xg_late = sb("xg_late", [P, 2, CHUNKS[3]], F32, on="xg_first")
+        for i in range(2):
+            gather_x(2 + i, spans[3], xg_late[:, i, :])
+        xb.append(sb("xb3", [P, CHUNKS[3], PACK], BF16, on="xb0"))
+        round_planes(0, 2, 3)
+        interleave(xb[3][:, :, 2:PACK], xg_late[:])
         quantize_x(1)
         product(0)
-        quantize_x(2)
+        quantize_x(2, on="yb0")
         quantize_h(0)
         product(1)
-        quantize_x(3)
+        quantize_x(3, on="yb2")
         quantize_h(1)
         wd_half(0)
         product(2)

@@ -49,17 +49,14 @@ def tile_list_htabg_mul_res_kernel(
         wa_s_raw = sb("wa_s_raw", [P, 128], I32)
         wb_w_raw = sb("wb_w_raw", [P, 2, 256], I32)
         wb_s_raw = sb("wb_s_raw", [P, 2, 128], I32)
-        wa_w = sb("wa_w", [P, PACK, 64], I32)
-        wa_s = sb("wa_s", [P, PACK, 32], I32)
-        wb_w = sb("wb_w", [P, PACK, 2, 64], I32)
         wb_s = sb("wb_s", [P, PACK, 2, 32], I32)
         wd_raw = sb("wd_raw", [P, PACK, N], F32)
         res_sb = sb("res_sb", [P, N // P, J], F32)
         v_pairs = sb("v_pairs", [P, J], U32)
-        v_w = sb("v_w", [P, 2, 2, 2 * HALF], U8)
+        v_w = [sb("v_w%d" % c, [P, 2, 2 * w], U8) for c, w in enumerate(CHUNKS)]
         v_s0 = sb("v_s0", [P, J], U8)
         v_s1 = sb("v_s1", [P, J // 4], I32)
-        yb = [sb("yb%d" % g, [P, GROUP, PACK], F32) for g in range(J // GROUP)]
+        yb = [sb("yb%d" % c, [P, 2, w, 2], F32) for c, w in enumerate(CHUNKS)]
         xg = sb("xg", [P, PACK, J], F32)
         xb = [sb("xb%d" % c, [P, w, PACK], BF16) for c, w in enumerate(CHUNKS[:-1])]
         wd_b = sb("wd_b", [P, N, PACK], BF16)
@@ -120,20 +117,11 @@ def tile_list_htabg_mul_res_kernel(
             cols = slice(half * HALF, (half + 1) * HALF)
             nc.sync.dma_start(res_sb[:, :, cols], res_rows[:, :, cols])
 
-        for half in range(2):
-            cols = slice(half * HALF, (half + 1) * HALF)
+        starts = [sum(CHUNKS[:c]) for c in range(len(CHUNKS))]
+        spans = [slice(s, s + w) for s, w in zip(starts, CHUNKS)]
+        for c, cols in enumerate(spans):
             nc.vector.tensor_copy(v_pairs[:, cols], tab_w[:].bitcast(U32).indirect(idx[:, entries(cols)]))
-        nc.vector.tensor_copy(
-            wb_w[:].rearrange("p t a (g e) -> p t (a g) e", e=4), wb_w_raw[:].rearrange("p a (g t e) -> p t (a g) e", t=PACK, e=4)
-        )
-        nc.vector.tensor_copy(
-            wb_s[:].rearrange("p t a (g e) -> p t (a g) e", e=2), wb_s_raw[:].rearrange("p a (g t e) -> p t (a g) e", t=PACK, e=2)
-        )
-        for half in range(2):
-            cols = slice(half * HALF, (half + 1) * HALF)
-            nc.vector.tensor_copy(
-                v_w[:, half].bitcast(U16), v_pairs[:, cols].bitcast(U16).rearrange("p (j a) -> p a j", a=2)
-            )
+            nc.vector.tensor_copy(v_w[c][:].bitcast(U16), v_pairs[:, cols].bitcast(U16).rearrange("p (j a) -> p a j", a=2))
         v_scales = (v_s0[:], v_s1[:].bitcast(U8))
 
         turned = psum.tile([P, P], F32, name="second")
@@ -147,28 +135,34 @@ def tile_list_htabg_mul_res_kernel(
                 nc.tensor.transpose(bank[:, b : b + P], wgt_wide[:, j0 + b : j0 + b + P], identity[:])
             nc.scalar.copy(wgt[:, j0 : j0 + 2 * P], bank[:])
 
-        for j0 in range(0, J, GROUP):
-            cols = slice(j0, j0 + GROUP)
-            half, within = divmod(j0, HALF)
-            bank = psum.tile([P, PACK, GROUP], F32, name="first")
-            for t in range(PACK):
-                for a in range(2):
-                    nc.tensor.matmul_mx(
-                        out=bank[:, t, :],
-                        lhsT=wb_w[:, t, a, :].bitcast(FP4X4),
-                        lhsT_scale=wb_s[:, t, a, :].bitcast(U8),
-                        rhs=v_w[:, half, a, 2 * within : 2 * (within + GROUP)].bitcast(FP4X4),
-                        rhs_scale=v_scales[a][:, cols],
-                        start=(a == 0),
-                        stop=(a == 1),
-                    )
-            nc.scalar.copy(yb[j0 // GROUP][:], bank[:].rearrange("p t j -> p j t"))
+        wb_w = sb("wb_w", [P, PACK, 2, 64], I32, on="wgt_wide")
+        nc.scalar.copy(
+            wb_w[:].bitcast(U32).rearrange("p t a (g e) -> p t (a g) e", e=4),
+            wb_w_raw[:].bitcast(U32).rearrange("p a (g t e) -> p t (a g) e", t=PACK, e=4),
+        )
+        nc.scalar.copy(
+            wb_s[:].bitcast(U32).rearrange("p t a (g e) -> p t (a g) e", e=2),
+            wb_s_raw[:].bitcast(U32).rearrange("p a (g t e) -> p t (a g) e", t=PACK, e=2),
+        )
+        for c, cols in enumerate(spans):
+            banks = [psum.tile([P, 2, CHUNKS[c]], F32, name="first") for u in range(2)]
+            for a in range(2):
+                for u in range(2):
+                    for e in range(2):
+                        nc.tensor.matmul_mx(
+                            out=banks[u][:, e, :],
+                            lhsT=wb_w[:, 2 * u + e, a, :].bitcast(FP4X4),
+                            lhsT_scale=wb_s[:, 2 * u + e, a, :].bitcast(U8),
+                            rhs=v_w[c][:, a, :].bitcast(FP4X4),
+                            rhs_scale=v_scales[a][:, cols],
+                            start=(a == 0 and e == 0),
+                            stop=(a == 1 and e == 1),
+                        )
+                    if a == 1:
+                        nc.scalar.copy(yb[c][:, u], banks[u][:].rearrange("p e j -> p j e"))
 
         def interleave(packed, planes):
             nc.scalar.copy(packed.rearrange("p (c e) t -> p c t e", e=4), planes.rearrange("p t (c e) -> p c t e", e=4))
-
-        starts = [sum(CHUNKS[:c]) for c in range(len(CHUNKS))]
-        spans = [slice(s, s + w) for s, w in zip(starts, CHUNKS)]
 
         def gather_x(i, cols, picked):
             nc.vector.tensor_tensor(picked, x_planes[i][:].indirect(idx2[:, entries(cols)]), wgt[:, cols], MULT)
@@ -182,11 +176,15 @@ def tile_list_htabg_mul_res_kernel(
             gather_x(i, spans[0], xg_first[:, i, :])
             gather_x(i, rest, xg[:, i, rest])
             if i == 1:
-                nc.vector.tensor_copy(
-                    wa_w[:].rearrange("p t (g e) -> p t g e", e=4), wa_w_raw[:].rearrange("p (g t e) -> p t g e", t=PACK, e=4)
+                wa_w = sb("wa_w", [P, PACK, 64], I32, on="wgt_wide")
+                wa_s = sb("wa_s", [P, PACK, 32], I32, on="wb_s")
+                nc.scalar.copy(
+                    wa_w[:].bitcast(U32).rearrange("p t (g e) -> p t g e", e=4),
+                    wa_w_raw[:].bitcast(U32).rearrange("p (g t e) -> p t g e", t=PACK, e=4),
                 )
-                nc.vector.tensor_copy(
-                    wa_s[:].rearrange("p t (g e) -> p t g e", e=2), wa_s_raw[:].rearrange("p (g t e) -> p t g e", t=PACK, e=2)
+                nc.scalar.copy(
+                    wa_s[:].bitcast(U32).rearrange("p t (g e) -> p t g e", e=2),
+                    wa_s_raw[:].bitcast(U32).rearrange("p (g t e) -> p t g e", t=PACK, e=2),
                 )
 
         middle = slice(spans[1].start, spans[2].stop)
@@ -211,7 +209,12 @@ def tile_list_htabg_mul_res_kernel(
                         start=True,
                         stop=True,
                     )
-                nc.vector.tensor_tensor(hb[c][:, within, :], bank[:].rearrange("p t j -> p j t"), yb[(spans[c].start + j0) // GROUP][:], MULT)
+                nc.vector.tensor_tensor(
+                    hb[c][:, within, :].rearrange("p j (u e) -> p j u e", e=2),
+                    bank[:].rearrange("p (u e) j -> p j u e", e=2),
+                    yb[c][:, :, within, :].rearrange("p u j e -> p j u e"),
+                    MULT,
+                )
 
         def second(c, b0):
             cols = spans[c]
@@ -273,10 +276,10 @@ def tile_list_htabg_mul_res_kernel(
         interleave(xb[3][:, :, 2:PACK], xg_late[:])
         quantize_x(1)
         product(0)
-        quantize_x(2, on="yb0")
+        quantize_x(2, on="x_packed0")
         quantize_h(0)
         product(1)
-        quantize_x(3, on="yb2")
+        quantize_x(3, on="x_packed1")
         quantize_h(1)
         wd_half(0)
         product(2)

@@ -20,9 +20,10 @@ ADD = mybir.AluOpType.add
 P = 128
 PACK = 4
 GROUP = 128
-HALF = J // 2
-CHUNKS = (256, 256, 256, 256)
-BANK = 512
+CHUNK = 256
+CHUNKS = J // CHUNK
+LEAD = 768
+EARLY_BANKS = 2
 
 
 def tile_list_htabg_mul_res_kernel(
@@ -35,6 +36,12 @@ def tile_list_htabg_mul_res_kernel(
 
         def sb(name, shape, dtype, on=""):
             return keep.tile(shape, dtype, name=name, tag=on or name, align_bytes=64)
+
+        def span(c, count=1):
+            return slice(c * CHUNK, (c + count) * CHUNK)
+
+        def entries(cols):
+            return slice(cols.start // 16, cols.stop // 16)
 
         idx = sb("idx", [P, J // 16], U16)
         idx2 = sb("idx2", [P, J // 16], U16)
@@ -49,79 +56,71 @@ def tile_list_htabg_mul_res_kernel(
         wa_s_raw = sb("wa_s_raw", [P, 128], I32)
         wb_w_raw = sb("wb_w_raw", [P, 2, 256], I32)
         wb_s_raw = sb("wb_s_raw", [P, 2, 128], I32)
-        wb_s = sb("wb_s", [P, PACK, 2, 32], I32)
-        wd_raw = sb("wd_raw", [P, PACK, N], F32)
-        res_sb = sb("res_sb", [P, N // P, J], F32)
+        wd_raw = [sb("wd_raw%d" % h, [P, PACK, N // 2], F32) for h in range(2)]
+        res_sb = [sb("res%d" % h, [P, N // P, J // 2], F32) for h in range(2)]
         v_pairs = sb("v_pairs", [P, J], U32)
-        v_w = [sb("v_w%d" % c, [P, 2, 2 * w], U8) for c, w in enumerate(CHUNKS)]
+        v_w = [sb("v_w%d" % c, [P, 2, 2 * CHUNK], U8) for c in range(CHUNKS)]
         v_s0 = sb("v_s0", [P, J], U8)
         v_s1 = sb("v_s1", [P, J // 4], I32)
-        yb = [sb("yb%d" % c, [P, 2, w, 2], F32) for c, w in enumerate(CHUNKS)]
-        xg = sb("xg", [P, PACK, J], F32)
-        xb = [sb("xb%d" % c, [P, w, PACK], BF16) for c, w in enumerate(CHUNKS[:-1])]
-        wd_b = sb("wd_b", [P, N, PACK], BF16)
-        wd_codes = sb("wd_codes", [P, N], U32)
-        wd_scales = sb("wd_scales", [P, N], U8)
-        hb = [sb("hb%d" % c, [P, w, PACK], BF16) for c, w in enumerate(CHUNKS)]
-        h_codes = sb("h_codes", [P, J], U32)
-        h_scales = sb("h_scales", [P, J], U8)
-        y_sb = sb("y_sb", [P, 2, 2, 256], F32)
-        out_sb = sb("out_sb", [P, N // P, J], F32)
+        yb = [sb("yb%d" % c, [P, 2, CHUNK, 2], F32) for c in range(CHUNKS)]
+        xg_first = sb("xg_first", [P, PACK, CHUNK], F32)
+        xg = sb("xg", [P, PACK, J - CHUNK], F32)
+        x_codes = [sb("x_codes%d" % c, [P, CHUNK], U32) for c in range(CHUNKS)]
+        x_scales = [sb("x_scales%d" % c, [P, CHUNK], U8) for c in range(CHUNKS)]
+        wd_codes = [sb("wd_codes%d" % h, [P, N // 2], U32) for h in range(2)]
+        wd_scales = [sb("wd_scales%d" % h, [P, N // 2], U8) for h in range(2)]
+        hb = [sb("hb%d" % c, [P, CHUNK, PACK], BF16) for c in range(CHUNKS)]
+        h_codes = [sb("h_codes%d" % c, [P, CHUNK], U32) for c in range(CHUNKS)]
+        h_scales = [sb("h_scales%d" % c, [P, CHUNK], U8) for c in range(CHUNKS)]
 
         nc.vector.memset(tab_s[:], 0)
-        nc.vector.memset(wb_s_raw[:], 0)
-        nc.vector.memset(wa_s_raw[:], 0)
-        nc.vector.memset(v_s1[:], 0)
         nc.vector.memset(wgt_rows[64:P, :], 0.0)
-        nc.vector.memset(identity[:], 0.0)
-        make_identity(nc, identity[:], nomemset=True)
+        nc.vector.memset(wb_s_raw[:], 0)
+        nc.vector.memset(v_s1[:], 0)
+        nc.vector.memset(wa_s_raw[:], 0)
+        make_identity(nc, identity[:])
 
         x_rows = xT.rearrange("(p i) t -> i p t", i=PACK)
         wd_rows = wd.rearrange("(g t q) n -> t g q n", t=PACK, q=8)
         res_rows = res.rearrange("(b p) j -> p b j", p=P)
         out_rows = out.rearrange("(b p) j -> p b j", p=P)
-
-        def entries(cols):
-            return slice(cols.start // 16, cols.stop // 16)
-
-        def quantize(codes, scales, values, cols):
-            nc.vector.quantize_mx(
-                out=codes[:, cols].bitcast(FP8X4), scales=scales[:, cols], in_=values[:, cols, :].rearrange("p j t -> p (j t)")
-            )
+        word_rows = tab_words[0].rearrange("p t b -> p (t b)").bitcast(I32)
+        tab_rows = tab_scales.rearrange("a (q s) t -> s q a t", s=4)
 
         nc.sync.dma_start(idx[:], offs)
         nc.sync.dma_start(wgt_rows[0:64, :], wgt2.rearrange("(g s) (b c) -> s b g c", s=16, c=P)[0])
-        tab_rows = tab_scales.rearrange("a (q s) t -> s q a t", s=4)
+        nc.sync.dma_start(tab_w[:, 0:LEAD], word_rows[:, 0:LEAD])
         for s in range(4):
             nc.sync.dma_start(tab_s[s:P:16, :], tab_rows[s].bitcast(I32))
-        nc.sync.dma_start(tab_w[:], tab_words[0].rearrange("p t b -> p (t b)").bitcast(I32))
+        nc.sync.dma_start(tab_w[:, LEAD:T], word_rows[:, LEAD:T])
         nc.sync.dma_start(wb_w_raw[:], wb_words.rearrange("a p c -> p a c").bitcast(I32))
         for q in range(4):
             nc.sync.dma_start(
                 wb_s_raw[32 * q : 32 * q + 4], wb_scales[:, 4 * q : 4 * q + 4, :].rearrange("a q c -> q a c").bitcast(I32)
             )
-        nc.sync.dma_start(idx2[:], offs2)
         nc.sync.dma_start(x_planes[0][:], x_rows[0])
+        nc.sync.dma_start(idx2[:], offs2)
         nc.vector.tensor_copy(v_s0[:], tab_s[:].bitcast(U8).indirect(idx[:]))
         for q in range(0, P, 32):
             nc.sync.dma_start(v_s1[q : q + 4, :], v_s0[q + 16 : q + 20, :].bitcast(I32))
         nc.sync.dma_start(x_planes[1][:], x_rows[1])
+        nc.sync.dma_start(wa_w_raw[:], wa_words[0].bitcast(I32))
         for q in range(4):
             nc.sync.dma_start(wa_s_raw[32 * q : 32 * q + 4, :], wa_scales[0, 4 * q : 4 * q + 4, :].bitcast(I32))
-        nc.sync.dma_start(wa_w_raw[:], wa_words[0].bitcast(I32))
         nc.sync.dma_start(x_planes[2][:], x_rows[2])
         nc.sync.dma_start(x_planes[3][:], x_rows[3])
-        for t in range(PACK):
-            nc.sync.dma_start(wd_raw[:, t, :], wd_rows[t])
-        for half in range(2):
-            cols = slice(half * HALF, (half + 1) * HALF)
-            nc.sync.dma_start(res_sb[:, :, cols], res_rows[:, :, cols])
+        for h in range(2):
+            for t in range(PACK):
+                nc.sync.dma_start(wd_raw[h][:, t, :], wd_rows[t][:, :, h * N // 2 : (h + 1) * N // 2])
+        for h in range(2):
+            nc.sync.dma_start(res_sb[h][:], res_rows[:, :, span(2 * h, 2)])
 
-        starts = [sum(CHUNKS[:c]) for c in range(len(CHUNKS))]
-        spans = [slice(s, s + w) for s, w in zip(starts, CHUNKS)]
-        for c, cols in enumerate(spans):
-            nc.vector.tensor_copy(v_pairs[:, cols], tab_w[:].bitcast(U32).indirect(idx[:, entries(cols)]))
-            nc.vector.tensor_copy(v_w[c][:].bitcast(U16), v_pairs[:, cols].bitcast(U16).rearrange("p (j a) -> p a j", a=2))
+        for c in range(CHUNKS):
+            nc.vector.tensor_copy(v_pairs[:, span(c)], tab_w[:].bitcast(U32).indirect(idx[:, entries(span(c))]))
+            nc.vector.tensor_copy(
+                v_w[c][:].bitcast(U16).rearrange("p a (m e) -> p m a e", e=8),
+                v_pairs[:, span(c)].bitcast(U16).rearrange("p (m e a) -> p m a e", e=8, a=2),
+            )
         v_scales = (v_s0[:], v_s1[:].bitcast(U8))
 
         turned = psum.tile([P, P], F32, name="second")
@@ -129,37 +128,42 @@ def tile_list_htabg_mul_res_kernel(
         nc.scalar.copy(
             wgt_wide[:].rearrange("p (m s) -> p m s", s=16), turned[:, 0:64].unsqueeze(2).to_broadcast([P, 64, 16])
         )
-        for j0 in range(0, J, 2 * P):
-            bank = psum.tile([P, 2 * P], F32, name="first")
-            for b in range(0, 2 * P, P):
-                nc.tensor.transpose(bank[:, b : b + P], wgt_wide[:, j0 + b : j0 + b + P], identity[:])
-            nc.scalar.copy(wgt[:, j0 : j0 + 2 * P], bank[:])
+        for c in range(CHUNKS):
+            bank = psum.tile([P, CHUNK], F32, name="first")
+            for b in range(0, CHUNK, P):
+                nc.tensor.transpose(bank[:, b : b + P], wgt_wide[:, c * CHUNK + b : c * CHUNK + b + P], identity[:])
+            nc.scalar.copy(wgt[:, span(c)], bank[:])
+
+        def regroup(grouped, raw, e):
+            nc.scalar.copy(
+                grouped.bitcast(U32).rearrange("p t (g e) -> p t g e", e=e),
+                raw.bitcast(U32).rearrange("p (g t e) -> p t g e", t=PACK, e=e),
+            )
 
         wb_w = sb("wb_w", [P, PACK, 2, 64], I32, on="wgt_wide")
-        nc.scalar.copy(
-            wb_w[:].bitcast(U32).rearrange("p t a (g e) -> p t (a g) e", e=4),
-            wb_w_raw[:].bitcast(U32).rearrange("p a (g t e) -> p t (a g) e", t=PACK, e=4),
-        )
-        nc.scalar.copy(
-            wb_s[:].bitcast(U32).rearrange("p t a (g e) -> p t (a g) e", e=2),
-            wb_s_raw[:].bitcast(U32).rearrange("p a (g t e) -> p t (a g) e", t=PACK, e=2),
-        )
-        for c, cols in enumerate(spans):
-            banks = [psum.tile([P, 2, CHUNKS[c]], F32, name="first") for u in range(2)]
-            for a in range(2):
-                for u in range(2):
+        wb_s = sb("wb_s", [P, PACK, 2, 32], I32, on="identity")
+        regroup(wb_w[:].rearrange("p t a c -> p t (a c)"), wb_w_raw[:].rearrange("p a c -> p (a c)"), 4)
+        regroup(wb_s[:].rearrange("p t a c -> p t (a c)"), wb_s_raw[:].rearrange("p a c -> p (a c)"), 2)
+        for c in range(CHUNKS):
+            for u in range(2):
+                bank = psum.tile([P, 2, CHUNK], F32, name="first")
+                order = (0, 1) if 2 * c + u < EARLY_BANKS else (1, 0)
+                for a in order:
                     for e in range(2):
                         nc.tensor.matmul_mx(
-                            out=banks[u][:, e, :],
+                            out=bank[:, e, :],
                             lhsT=wb_w[:, 2 * u + e, a, :].bitcast(FP4X4),
                             lhsT_scale=wb_s[:, 2 * u + e, a, :].bitcast(U8),
                             rhs=v_w[c][:, a, :].bitcast(FP4X4),
-                            rhs_scale=v_scales[a][:, cols],
-                            start=(a == 0 and e == 0),
-                            stop=(a == 1 and e == 1),
+                            rhs_scale=v_scales[a][:, span(c)],
+                            start=(a == order[0] and e == 0),
+                            stop=(a == order[1] and e == 1),
                         )
-                    if a == 1:
-                        nc.scalar.copy(yb[c][:, u], banks[u][:].rearrange("p e j -> p j e"))
+                nc.scalar.copy(yb[c][:, u], bank[:].rearrange("p e j -> p j e"))
+        wa_w = sb("wa_w", [P, PACK, 64], I32, on="wgt_wide")
+        wa_s = sb("wa_s", [P, PACK, 32], I32, on="identity")
+        regroup(wa_w[:], wa_w_raw[:], 4)
+        regroup(wa_s[:], wa_s_raw[:], 2)
 
         def interleave(packed, planes):
             nc.scalar.copy(packed.rearrange("p (c e) t -> p c t e", e=4), planes.rearrange("p t (c e) -> p c t e", e=4))
@@ -167,36 +171,30 @@ def tile_list_htabg_mul_res_kernel(
         def gather_x(i, cols, picked):
             nc.vector.tensor_tensor(picked, x_planes[i][:].indirect(idx2[:, entries(cols)]), wgt[:, cols], MULT)
 
-        def round_planes(first, stop, c):
-            interleave(xb[c][:, :, first:stop], xg[:, first:stop, spans[c]])
+        def quantize(codes, scales, values):
+            nc.vector.quantize_mx(out=codes[:].bitcast(FP8X4), scales=scales[:], in_=values[:].rearrange("p j t -> p (j t)"))
 
-        xg_first = sb("xg_first", [P, PACK, CHUNKS[0]], F32)
-        rest = slice(spans[1].start, J)
+        last = CHUNKS - 1
+        xb = [sb("xb%d" % c, [P, CHUNK, PACK], BF16, on="v_w3" if c == last else "") for c in range(CHUNKS)]
         for i in range(2):
-            gather_x(i, spans[0], xg_first[:, i, :])
-            gather_x(i, rest, xg[:, i, rest])
-            if i == 1:
-                wa_w = sb("wa_w", [P, PACK, 64], I32, on="wgt_wide")
-                wa_s = sb("wa_s", [P, PACK, 32], I32, on="wb_s")
-                nc.scalar.copy(
-                    wa_w[:].bitcast(U32).rearrange("p t (g e) -> p t g e", e=4),
-                    wa_w_raw[:].bitcast(U32).rearrange("p (g t e) -> p t g e", t=PACK, e=4),
-                )
-                nc.scalar.copy(
-                    wa_s[:].bitcast(U32).rearrange("p t (g e) -> p t g e", e=2),
-                    wa_s_raw[:].bitcast(U32).rearrange("p (g t e) -> p t g e", t=PACK, e=2),
-                )
+            gather_x(i, span(0), xg_first[:, i, :])
+            gather_x(i, span(1, last), xg[:, i, :])
+        interleave(xb[last][:, :, 0:2], xg[:, 0:2, span(last - 1)])
+        for i in range(2, PACK):
+            gather_x(i, span(0), xg_first[:, i, :])
+            gather_x(i, span(1, 2), xg[:, i, span(0, 2)])
 
-        middle = slice(spans[1].start, spans[2].stop)
-        gather_x(2, spans[0], xg_first[:, 2, :])
-        gather_x(2, middle, xg[:, 2, middle])
+        def quantize_x(c):
+            quantize(x_codes[c], x_scales[c], xb[c])
 
-        def last_plane(c):
-            gather_x(PACK - 1, spans[c], xg[:, PACK - 1, spans[c]])
-            round_planes(0, PACK, c)
+        def quantize_h(c):
+            quantize(h_codes[c], h_scales[c], hb[c])
+
+        def quantize_wd(h):
+            quantize(wd_codes[h], wd_scales[h], wd_b[h])
 
         def product(c):
-            for j0 in range(0, CHUNKS[c], GROUP):
+            for j0 in range(0, CHUNK, GROUP):
                 within = slice(j0, j0 + GROUP)
                 bank = psum.tile([P, PACK, GROUP], F32, name="first")
                 for t in range(PACK):
@@ -216,88 +214,68 @@ def tile_list_htabg_mul_res_kernel(
                     MULT,
                 )
 
-        def second(c, b0):
-            cols = spans[c]
-            bank = psum.tile([P, 2, cols.stop - cols.start], F32, name="second")
+        def second(c, h):
+            bank = psum.tile([P, 2, CHUNK], F32, name="second")
             for b in range(2):
-                n_cols = slice((b0 + b) * P, (b0 + b + 1) * P)
                 nc.tensor.matmul_mx(
                     out=bank[:, b, :],
-                    lhsT=wd_codes[:, n_cols].bitcast(FP8X4),
-                    lhsT_scale=wd_scales[:, n_cols],
-                    rhs=h_codes[:, cols].bitcast(FP8X4),
-                    rhs_scale=h_scales[:, cols],
+                    lhsT=wd_codes[h][:, b * P : (b + 1) * P].bitcast(FP8X4),
+                    lhsT_scale=wd_scales[h][:, b * P : (b + 1) * P],
+                    rhs=h_codes[c][:].bitcast(FP8X4),
+                    rhs_scale=h_scales[c][:],
                     start=True,
                     stop=True,
                 )
             return bank
 
-        def finish(c, b0):
-            cols, blocks = spans[c], slice(b0, b0 + 2)
-            nc.vector.tensor_tensor(out_sb[:, blocks, cols], second(c, b0)[:], res_sb[:, blocks, cols], ADD)
-            nc.sync.dma_start(out_rows[:, blocks, cols], out_sb[:, blocks, cols])
+        def residual(c, h):
+            return res_sb[c // 2][:, 2 * h : 2 * h + 2, span(c % 2)]
 
-        def copy_out(c, b0, k):
-            nc.scalar.copy(y_sb[:, k], second(c, b0)[:])
+        def finish(c, h):
+            sums = sb("sums%d%d" % (c, h), [P, 2, CHUNK], F32)
+            nc.vector.tensor_tensor(sums[:], second(c, h)[:], residual(c, h), ADD)
+            nc.sync.dma_start(out_rows[:, 2 * h : 2 * h + 2, span(c)], sums[:])
 
-        def finish_on_gpsimd(c, b0, k, sums):
-            for b in range(2):
-                nc.gpsimd.tensor_tensor(sums[:, b, :], y_sb[:, k, b, :], res_sb[:, b0 + b, spans[c]], ADD)
-            nc.scalar.dma_start(out_rows[:, b0 : b0 + 2, spans[c]], sums)
+        def finish_on_gpsimd(c, h, on):
+            y_sb = sb("y_sb%d%d" % (c, h), [P, 2, CHUNK], F32)
+            nc.scalar.copy(y_sb[:], second(c, h)[:])
+            sums = sb("sums%d%d" % (c, h), [P, 2, CHUNK], F32, on=on)
+            nc.gpsimd.tensor_tensor(sums[:], y_sb[:], residual(c, h), ADD)
+            nc.scalar.dma_start(out_rows[:, 2 * h : 2 * h + 2, span(c)], sums[:])
 
-        def wd_half(half):
-            n_cols = slice(half * N // 2, (half + 1) * N // 2)
-            interleave(wd_b[:, n_cols, :], wd_raw[:, :, n_cols])
-            quantize(wd_codes, wd_scales, wd_b, n_cols)
-
-        x_codes, x_scales = [], []
-
-        def quantize_x(c, on=""):
-            packed = sb("x_packed%d" % c, [P, CHUNKS[c] + CHUNKS[c] // 4], I32, on=on)
-            x_codes.append(packed[:, 0 : CHUNKS[c]])
-            x_scales.append(packed[:, CHUNKS[c] :].bitcast(U8))
-            nc.vector.quantize_mx(out=x_codes[c].bitcast(FP8X4), scales=x_scales[c], in_=xb[c][:].rearrange("p j t -> p (j t)"))
-
-        def quantize_h(c):
-            nc.vector.quantize_mx(
-                out=h_codes[:, spans[c]].bitcast(FP8X4), scales=h_scales[:, spans[c]], in_=hb[c][:].rearrange("p j t -> p (j t)")
-            )
-
-        gather_x(PACK - 1, spans[0], xg_first[:, PACK - 1, :])
         interleave(xb[0][:], xg_first[:])
-        last_plane(1)
-        last_plane(2)
         quantize_x(0)
-        xg_late = sb("xg_late", [P, 2, CHUNKS[3]], F32, on="xg_first")
+        xg_late = sb("xg_late", [P, 2, CHUNK], F32, on="xg_first")
         for i in range(2):
-            gather_x(2 + i, spans[3], xg_late[:, i, :])
-        xb.append(sb("xb3", [P, CHUNKS[3], PACK], BF16, on="xb0"))
-        round_planes(0, 2, 3)
-        interleave(xb[3][:, :, 2:PACK], xg_late[:])
+            gather_x(2 + i, span(last), xg_late[:, i, :])
+        interleave(xb[1][:], xg[:, :, span(0)])
         quantize_x(1)
+        wd_b = [sb("wd_b%d" % h, [P, N // 2, PACK], BF16, on="xb%d" % h) for h in range(2)]
+        interleave(wd_b[0][:], wd_raw[0][:])
+        interleave(xb[2][:], xg[:, :, span(1)])
+        interleave(xb[last][:, :, 2:PACK], xg_late[:])
+        interleave(wd_b[1][:], wd_raw[1][:])
         product(0)
-        quantize_x(2, on="x_packed0")
+        quantize_wd(0)
         quantize_h(0)
+        quantize_x(2)
         product(1)
-        quantize_x(3, on="x_packed1")
+        quantize_x(3)
         quantize_h(1)
-        wd_half(0)
+        quantize_wd(1)
+        finish_on_gpsimd(0, 0, "xb1")
         product(2)
-        wd_half(1)
-        copy_out(0, 0, 0)
-        quantize_h(2)
         finish(1, 0)
-        copy_out(0, 2, 1)
-        sums0 = sb("sums0", [P, 4, 256], F32, on="hb2")
-        finish_on_gpsimd(0, 0, 0, sums0[:, 0:2, :])
+        quantize_h(2)
+        finish_on_gpsimd(0, 1, "hb2")
         product(3)
-        finish(1, 2)
-        finish_on_gpsimd(0, 2, 1, sums0[:, 2:4, :])
-        finish(2, 0)
+        finish(1, 1)
         quantize_h(3)
-        finish(2, 2)
+        finish(2, 0)
+        finish(2, 1)
         finish(3, 0)
-        last = second(3, 2)
+        bank = second(last, 1)
         for b in range(2):
-            nc.vector.tensor_tensor(out_sb[:, 2 + b, spans[3]], last[:, b, :], res_sb[:, 2 + b, spans[3]], ADD)
-            (nc.sync, nc.scalar)[b].dma_start(out_rows[:, 2 + b, spans[3]], out_sb[:, 2 + b, spans[3]])
+            sums = sb("sums_last%d" % b, [P, CHUNK], F32)
+            nc.vector.tensor_tensor(sums[:], bank[:, b, :], residual(last, 1)[:, b, :], ADD)
+            (nc.sync, nc.scalar)[b].dma_start(out_rows[:, 2 + b, span(last)], sums[:])

@@ -22,7 +22,6 @@ PACK = 4
 GROUP = 128
 CHUNK = 256
 CHUNKS = J // CHUNK
-LEAD = 768
 EARLY_BANKS = 2
 
 
@@ -32,7 +31,8 @@ def tile_list_htabg_mul_res_kernel(
     nc = tc.nc
     with ExitStack() as ctx:
         keep = ctx.enter_context(tc.tile_pool(name="keep", bufs=1))
-        psum = ctx.enter_context(tc.psum_pool(name="psum", bufs=4))
+        psum = ctx.enter_context(tc.psum_pool(name="psum", bufs=3))
+        psum_late = ctx.enter_context(tc.psum_pool(name="psum_late", bufs=5))
 
         def sb(name, shape, dtype, on=""):
             return keep.tile(shape, dtype, name=name, tag=on or name, align_bytes=64)
@@ -56,13 +56,13 @@ def tile_list_htabg_mul_res_kernel(
         wa_s_raw = sb("wa_s_raw", [P, 128], I32)
         wb_w_raw = sb("wb_w_raw", [P, 2, 256], I32)
         wb_s_raw = sb("wb_s_raw", [P, 2, 128], I32)
-        wd_raw = [sb("wd_raw%d" % h, [P, PACK, N // 2], F32) for h in range(2)]
+        wd_raw = sb("wd_raw", [P, PACK, N], F32)
         res_sb = [sb("res%d" % h, [P, N // P, J // 2], F32) for h in range(2)]
         v_pairs = sb("v_pairs", [P, J], U32)
         v_w = [sb("v_w%d" % c, [P, 2, 2 * CHUNK], U8) for c in range(CHUNKS)]
         v_s0 = sb("v_s0", [P, J], U8)
         v_s1 = sb("v_s1", [P, J // 4], I32)
-        yb = [sb("yb%d" % c, [P, 2, CHUNK, 2], F32) for c in range(CHUNKS)]
+        yb = [sb("yb%d" % c, [P, 2, CHUNK, 2], F32) for c in range(CHUNKS - 1)]
         xg_first = sb("xg_first", [P, PACK, CHUNK], F32)
         xg = sb("xg", [P, PACK, J - CHUNK], F32)
         x_codes = [sb("x_codes%d" % c, [P, CHUNK], U32) for c in range(CHUNKS)]
@@ -89,17 +89,16 @@ def tile_list_htabg_mul_res_kernel(
 
         nc.sync.dma_start(idx[:], offs)
         nc.sync.dma_start(wgt_rows[0:64, :], wgt2.rearrange("(g s) (b c) -> s b g c", s=16, c=P)[0])
-        nc.sync.dma_start(tab_w[:, 0:LEAD], word_rows[:, 0:LEAD])
         for s in range(4):
             nc.sync.dma_start(tab_s[s:P:16, :], tab_rows[s].bitcast(I32))
-        nc.sync.dma_start(tab_w[:, LEAD:T], word_rows[:, LEAD:T])
+        nc.sync.dma_start(tab_w[:], word_rows)
         nc.sync.dma_start(wb_w_raw[:], wb_words.rearrange("a p c -> p a c").bitcast(I32))
         for q in range(4):
             nc.sync.dma_start(
                 wb_s_raw[32 * q : 32 * q + 4], wb_scales[:, 4 * q : 4 * q + 4, :].rearrange("a q c -> q a c").bitcast(I32)
             )
-        nc.sync.dma_start(x_planes[0][:], x_rows[0])
         nc.sync.dma_start(idx2[:], offs2)
+        nc.sync.dma_start(x_planes[0][:], x_rows[0])
         nc.vector.tensor_copy(v_s0[:], tab_s[:].bitcast(U8).indirect(idx[:]))
         for q in range(0, P, 32):
             nc.sync.dma_start(v_s1[q : q + 4, :], v_s0[q + 16 : q + 20, :].bitcast(I32))
@@ -109,21 +108,17 @@ def tile_list_htabg_mul_res_kernel(
             nc.sync.dma_start(wa_s_raw[32 * q : 32 * q + 4, :], wa_scales[0, 4 * q : 4 * q + 4, :].bitcast(I32))
         nc.sync.dma_start(x_planes[2][:], x_rows[2])
         nc.sync.dma_start(x_planes[3][:], x_rows[3])
-        for h in range(2):
-            for t in range(PACK):
-                nc.sync.dma_start(wd_raw[h][:, t, :], wd_rows[t][:, :, h * N // 2 : (h + 1) * N // 2])
+        for t in range(PACK):
+            nc.sync.dma_start(wd_raw[:, t, :], wd_rows[t])
         for h in range(2):
             nc.sync.dma_start(res_sb[h][:], res_rows[:, :, span(2 * h, 2)])
 
         for c in range(CHUNKS):
             nc.vector.tensor_copy(v_pairs[:, span(c)], tab_w[:].bitcast(U32).indirect(idx[:, entries(span(c))]))
-            nc.vector.tensor_copy(
-                v_w[c][:].bitcast(U16).rearrange("p a (m e) -> p m a e", e=8),
-                v_pairs[:, span(c)].bitcast(U16).rearrange("p (m e a) -> p m a e", e=8, a=2),
-            )
+            nc.vector.tensor_copy(v_w[c][:].bitcast(U16), v_pairs[:, span(c)].bitcast(U16).rearrange("p (j a) -> p a j", a=2))
         v_scales = (v_s0[:], v_s1[:].bitcast(U8))
 
-        turned = psum.tile([P, P], F32, name="second")
+        turned = psum_late.tile([P, P], F32, name="second")
         nc.tensor.transpose(turned[:], wgt_rows[:], identity[:])
         nc.scalar.copy(
             wgt_wide[:].rearrange("p (m s) -> p m s", s=16), turned[:, 0:64].unsqueeze(2).to_broadcast([P, 64, 16])
@@ -144,9 +139,15 @@ def tile_list_htabg_mul_res_kernel(
         wb_s = sb("wb_s", [P, PACK, 2, 32], I32, on="identity")
         regroup(wb_w[:].rearrange("p t a c -> p t (a c)"), wb_w_raw[:].rearrange("p a c -> p (a c)"), 4)
         regroup(wb_s[:].rearrange("p t a c -> p t (a c)"), wb_s_raw[:].rearrange("p a c -> p (a c)"), 2)
+        last = CHUNKS - 1
+        held = []
+
+        def copy_yb(c, u, bank):
+            nc.scalar.copy(yb[c][:, u], bank[:].rearrange("p e j -> p j e"))
+
         for c in range(CHUNKS):
             for u in range(2):
-                bank = psum.tile([P, 2, CHUNK], F32, name="first")
+                bank = (psum if c < last else psum_late).tile([P, 2, CHUNK], F32, name="first" if c < last else "second")
                 order = (0, 1) if 2 * c + u < EARLY_BANKS else (1, 0)
                 for a in order:
                     for e in range(2):
@@ -159,7 +160,10 @@ def tile_list_htabg_mul_res_kernel(
                             start=(a == order[0] and e == 0),
                             stop=(a == order[1] and e == 1),
                         )
-                nc.scalar.copy(yb[c][:, u], bank[:].rearrange("p e j -> p j e"))
+                if c < last:
+                    copy_yb(c, u, bank)
+                else:
+                    held.append(bank)
         wa_w = sb("wa_w", [P, PACK, 64], I32, on="wgt_wide")
         wa_s = sb("wa_s", [P, PACK, 32], I32, on="identity")
         regroup(wa_w[:], wa_w_raw[:], 4)
@@ -174,8 +178,7 @@ def tile_list_htabg_mul_res_kernel(
         def quantize(codes, scales, values):
             nc.vector.quantize_mx(out=codes[:].bitcast(FP8X4), scales=scales[:], in_=values[:].rearrange("p j t -> p (j t)"))
 
-        last = CHUNKS - 1
-        xb = [sb("xb%d" % c, [P, CHUNK, PACK], BF16, on="v_w3" if c == last else "") for c in range(CHUNKS)]
+        xb = [sb("xb%d" % c, [P, CHUNK, PACK], BF16, on="wa_s_raw" if c == last else "") for c in range(CHUNKS)]
         for i in range(2):
             gather_x(i, span(0), xg_first[:, i, :])
             gather_x(i, span(1, last), xg[:, i, :])
@@ -193,29 +196,28 @@ def tile_list_htabg_mul_res_kernel(
         def quantize_wd(h):
             quantize(wd_codes[h], wd_scales[h], wd_b[h])
 
-        def product(c):
-            for j0 in range(0, CHUNK, GROUP):
-                within = slice(j0, j0 + GROUP)
-                bank = psum.tile([P, PACK, GROUP], F32, name="first")
-                for t in range(PACK):
-                    nc.tensor.matmul_mx(
-                        out=bank[:, t, :],
-                        lhsT=wa_w[:, t, :].bitcast(FP4X4),
-                        lhsT_scale=wa_s[:, t, :].bitcast(U8),
-                        rhs=x_codes[c][:, within].bitcast(FP8X4),
-                        rhs_scale=x_scales[c][:, within],
-                        start=True,
-                        stop=True,
-                    )
-                nc.vector.tensor_tensor(
-                    hb[c][:, within, :].rearrange("p j (u e) -> p j u e", e=2),
-                    bank[:].rearrange("p (u e) j -> p j u e", e=2),
-                    yb[c][:, :, within, :].rearrange("p u j e -> p j u e"),
-                    MULT,
+        def product(c, g):
+            within = slice(g * GROUP, (g + 1) * GROUP)
+            bank = psum.tile([P, PACK, GROUP], F32, name="first")
+            for t in range(PACK):
+                nc.tensor.matmul_mx(
+                    out=bank[:, t, :],
+                    lhsT=wa_w[:, t, :].bitcast(FP4X4),
+                    lhsT_scale=wa_s[:, t, :].bitcast(U8),
+                    rhs=x_codes[c][:, within].bitcast(FP8X4),
+                    rhs_scale=x_scales[c][:, within],
+                    start=True,
+                    stop=True,
                 )
+            nc.vector.tensor_tensor(
+                hb[c][:, within, :].rearrange("p j (u e) -> p j u e", e=2),
+                bank[:].rearrange("p (u e) j -> p j u e", e=2),
+                yb[c][:, :, within, :].rearrange("p u j e -> p j u e"),
+                MULT,
+            )
 
         def second(c, h):
-            bank = psum.tile([P, 2, CHUNK], F32, name="second")
+            bank = psum_late.tile([P, 2, CHUNK], F32, name="second")
             for b in range(2):
                 nc.tensor.matmul_mx(
                     out=bank[:, b, :],
@@ -241,7 +243,7 @@ def tile_list_htabg_mul_res_kernel(
             nc.scalar.copy(y_sb[:], second(c, h)[:])
             sums = sb("sums%d%d" % (c, h), [P, 2, CHUNK], F32, on=on)
             nc.gpsimd.tensor_tensor(sums[:], y_sb[:], residual(c, h), ADD)
-            nc.scalar.dma_start(out_rows[:, 2 * h : 2 * h + 2, span(c)], sums[:])
+            nc.sync.dma_start(out_rows[:, 2 * h : 2 * h + 2, span(c)], sums[:])
 
         interleave(xb[0][:], xg_first[:])
         quantize_x(0)
@@ -250,28 +252,35 @@ def tile_list_htabg_mul_res_kernel(
             gather_x(2 + i, span(last), xg_late[:, i, :])
         interleave(xb[1][:], xg[:, :, span(0)])
         quantize_x(1)
-        wd_b = [sb("wd_b%d" % h, [P, N // 2, PACK], BF16, on="xb%d" % h) for h in range(2)]
-        interleave(wd_b[0][:], wd_raw[0][:])
         interleave(xb[2][:], xg[:, :, span(1)])
         interleave(xb[last][:, :, 2:PACK], xg_late[:])
-        interleave(wd_b[1][:], wd_raw[1][:])
-        product(0)
-        quantize_wd(0)
-        quantize_h(0)
+        wd_b = [sb("wd_b%d" % h, [P, N // 2, PACK], BF16, on="xb%d" % h) for h in range(2)]
+        for h in range(2):
+            interleave(wd_b[h][:], wd_raw[:, :, h * N // 2 : (h + 1) * N // 2])
+        product(0, 0)
+        product(0, 1)
         quantize_x(2)
-        product(1)
+        quantize_h(0)
         quantize_x(3)
-        quantize_h(1)
+        product(1, 0)
+        quantize_wd(0)
+        product(1, 1)
         quantize_wd(1)
-        finish_on_gpsimd(0, 0, "xb1")
-        product(2)
+        quantize_h(1)
+        finish_on_gpsimd(0, 0, "hb1")
+        yb.append(sb("yb3", [P, 2, CHUNK, 2], F32, on="wd_raw"))
+        for u in range(2):
+            copy_yb(last, u, held[u])
+        product(2, 0)
+        product(2, 1)
         finish(1, 0)
+        finish(1, 1)
         quantize_h(2)
         finish_on_gpsimd(0, 1, "hb2")
-        product(3)
-        finish(1, 1)
-        quantize_h(3)
+        product(3, 0)
+        product(3, 1)
         finish(2, 0)
+        quantize_h(3)
         finish(2, 1)
         finish(3, 0)
         bank = second(last, 1)

@@ -22,7 +22,6 @@ PACK = 4
 GROUP = 128
 CHUNK = 256
 CHUNKS = J // CHUNK
-EARLY_BANKS = 2
 
 
 def tile_list_htabg_mul_res_kernel(
@@ -60,8 +59,8 @@ def tile_list_htabg_mul_res_kernel(
         res_sb = [sb("res%d" % h, [P, N // P, J // 2], F32) for h in range(2)]
         v_pairs = sb("v_pairs", [P, J], U32)
         v_w = [sb("v_w%d" % c, [P, 2, 2 * CHUNK], U8) for c in range(CHUNKS)]
-        v_s0 = sb("v_s0", [P, J], U8)
-        v_s1 = sb("v_s1", [P, J // 4], I32)
+        v_rows = sb("v_rows", [P, J], U8)
+        v_s = sb("v_s", [P, 2, J // 4], I32)
         yb = [sb("yb%d" % c, [P, 2, CHUNK, 2], F32) for c in range(CHUNKS - 1)]
         xg_first = sb("xg_first", [P, PACK, CHUNK], F32)
         xg = sb("xg", [P, PACK, J - CHUNK], F32)
@@ -73,35 +72,37 @@ def tile_list_htabg_mul_res_kernel(
         h_codes = [sb("h_codes%d" % c, [P, CHUNK], U32) for c in range(CHUNKS)]
         h_scales = [sb("h_scales%d" % c, [P, CHUNK], U8) for c in range(CHUNKS)]
 
-        nc.vector.memset(tab_s[:], 0)
-        nc.vector.memset(wgt_rows[64:P, :], 0.0)
         nc.vector.memset(wb_s_raw[:], 0)
-        nc.vector.memset(v_s1[:], 0)
-        nc.vector.memset(wa_s_raw[:], 0)
+        nc.vector.memset(tab_s[32:64, :], 0)
+        nc.vector.memset(tab_s[64:P, :], 0)
+        nc.vector.memset(wgt_rows[64:P, :], 0.0)
         make_identity(nc, identity[:])
+        nc.gpsimd.memset(v_s[:], 0)
+        nc.gpsimd.memset(wa_s_raw[:], 0)
 
         x_rows = xT.rearrange("(p i) t -> i p t", i=PACK)
         wd_rows = wd.rearrange("(g t q) n -> t g q n", t=PACK, q=8)
         res_rows = res.rearrange("(b p) j -> p b j", p=P)
         out_rows = out.rearrange("(b p) j -> p b j", p=P)
         word_rows = tab_words[0].rearrange("p t b -> p (t b)").bitcast(I32)
-        tab_rows = tab_scales.rearrange("a (q s) t -> s q a t", s=4)
+        tab_rows = tab_scales.rearrange("a m t -> m a t")
 
+        nc.sync.dma_start(tab_s[0:32, :], tab_rows.bitcast(I32))
+        nc.scalar.dma_start(wgt_rows[0:64, :], wgt2.rearrange("(g s) (b c) -> s b g c", s=16, c=P)[0])
         nc.sync.dma_start(idx[:], offs)
-        nc.sync.dma_start(wgt_rows[0:64, :], wgt2.rearrange("(g s) (b c) -> s b g c", s=16, c=P)[0])
-        for s in range(4):
-            nc.sync.dma_start(tab_s[s:P:16, :], tab_rows[s].bitcast(I32))
         nc.sync.dma_start(tab_w[:], word_rows)
         nc.sync.dma_start(wb_w_raw[:], wb_words.rearrange("a p c -> p a c").bitcast(I32))
         for q in range(4):
             nc.sync.dma_start(
                 wb_s_raw[32 * q : 32 * q + 4], wb_scales[:, 4 * q : 4 * q + 4, :].rearrange("a q c -> q a c").bitcast(I32)
             )
-        nc.sync.dma_start(idx2[:], offs2)
         nc.sync.dma_start(x_planes[0][:], x_rows[0])
-        nc.vector.tensor_copy(v_s0[:], tab_s[:].bitcast(U8).indirect(idx[:]))
-        for q in range(0, P, 32):
-            nc.sync.dma_start(v_s1[q : q + 4, :], v_s0[q + 16 : q + 20, :].bitcast(I32))
+        nc.vector.tensor_copy(v_rows[:], tab_s[:].bitcast(U8).indirect(idx[:]))
+        for q in range(4):
+            nc.sync.dma_start(
+                v_s[32 * q : 32 * q + 4].rearrange("p a c -> p (a c)"), v_rows[8 * q : 8 * q + 8, :].bitcast(I32)
+            )
+        nc.sync.dma_start(idx2[:], offs2)
         nc.sync.dma_start(x_planes[1][:], x_rows[1])
         nc.sync.dma_start(wa_w_raw[:], wa_words[0].bitcast(I32))
         for q in range(4):
@@ -116,7 +117,7 @@ def tile_list_htabg_mul_res_kernel(
         for c in range(CHUNKS):
             nc.vector.tensor_copy(v_pairs[:, span(c)], tab_w[:].bitcast(U32).indirect(idx[:, entries(span(c))]))
             nc.vector.tensor_copy(v_w[c][:].bitcast(U16), v_pairs[:, span(c)].bitcast(U16).rearrange("p (j a) -> p a j", a=2))
-        v_scales = (v_s0[:], v_s1[:].bitcast(U8))
+        v_scales = [v_s[:, a, :].bitcast(U8) for a in range(2)]
 
         turned = psum_late.tile([P, P], F32, name="second")
         nc.tensor.transpose(turned[:], wgt_rows[:], identity[:])
@@ -148,8 +149,7 @@ def tile_list_htabg_mul_res_kernel(
         for c in range(CHUNKS):
             for u in range(2):
                 bank = (psum if c < last else psum_late).tile([P, 2, CHUNK], F32, name="first" if c < last else "second")
-                order = (0, 1) if 2 * c + u < EARLY_BANKS else (1, 0)
-                for a in order:
+                for a in range(2):
                     for e in range(2):
                         nc.tensor.matmul_mx(
                             out=bank[:, e, :],
@@ -157,8 +157,8 @@ def tile_list_htabg_mul_res_kernel(
                             lhsT_scale=wb_s[:, 2 * u + e, a, :].bitcast(U8),
                             rhs=v_w[c][:, a, :].bitcast(FP4X4),
                             rhs_scale=v_scales[a][:, span(c)],
-                            start=(a == order[0] and e == 0),
-                            stop=(a == order[1] and e == 1),
+                            start=(a == 0 and e == 0),
+                            stop=(a == 1 and e == 1),
                         )
                 if c < last:
                     copy_yb(c, u, bank)

@@ -30,11 +30,15 @@ def tile_list_htabg_mul_res_kernel(
     nc = tc.nc
     with ExitStack() as ctx:
         keep = ctx.enter_context(tc.tile_pool(name="keep", bufs=1))
+        shared = ctx.enter_context(tc.tile_pool(name="shared", bufs=1))
         psum = ctx.enter_context(tc.psum_pool(name="psum", bufs=3))
         psum_late = ctx.enter_context(tc.psum_pool(name="psum_late", bufs=5))
 
         def sb(name, shape, dtype, on=""):
             return keep.tile(shape, dtype, name=name, tag=on or name, align_bytes=64)
+
+        def placed(name, shape, dtype, offset):
+            return shared.tile(shape, dtype, name=name, align_bytes=64, offset=offset)
 
         def span(c, count=1):
             return slice(c * CHUNK, (c + count) * CHUNK)
@@ -58,12 +62,15 @@ def tile_list_htabg_mul_res_kernel(
         wd_raw = sb("wd_raw", [P, PACK, N], F32)
         res_sb = [sb("res%d" % h, [P, N // P, J // 2], F32) for h in range(2)]
         v_pairs = sb("v_pairs", [P, J], U32)
-        v_w = [sb("v_w%d" % c, [P, 2, 2 * CHUNK], U8) for c in range(CHUNKS)]
+        v_w = [
+            placed("v_w2", [P, 2, 2 * CHUNK], U8, 1536) if c == 2 else sb("v_w%d" % c, [P, 2, 2 * CHUNK], U8)
+            for c in range(CHUNKS)
+        ]
         v_rows = sb("v_rows", [P, J], U8)
         v_s = sb("v_s", [P, 2, J // 4], I32)
         yb = [sb("yb%d" % c, [P, 2, CHUNK, 2], F32) for c in range(CHUNKS - 1)]
-        xg_first = sb("xg_first", [P, PACK, CHUNK], F32)
-        xg = sb("xg", [P, PACK, J - CHUNK], F32)
+        xg_first = sb("xg_first", [P, 2, CHUNK], F32)
+        xg = sb("xg", [P, PACK, J], F32)
         x_codes = [sb("x_codes%d" % c, [P, CHUNK], U32) for c in range(CHUNKS)]
         x_scales = [sb("x_scales%d" % c, [P, CHUNK], U8) for c in range(CHUNKS)]
         wd_codes = [sb("wd_codes%d" % h, [P, N // 2], U32) for h in range(2)]
@@ -178,14 +185,21 @@ def tile_list_htabg_mul_res_kernel(
         def quantize(codes, scales, values):
             nc.vector.quantize_mx(out=codes[:].bitcast(FP8X4), scales=scales[:], in_=values[:].rearrange("p j t -> p (j t)"))
 
-        xb = [sb("xb%d" % c, [P, CHUNK, PACK], BF16, on="wa_s_raw" if c == last else "") for c in range(CHUNKS)]
+        xb = [
+            placed("xb0", [P, CHUNK, PACK], BF16, 0),
+            sb("xb1", [P, CHUNK, PACK], BF16),
+            sb("xb2", [P, CHUNK, PACK], BF16),
+            placed("xb3", [P, CHUNK, PACK], BF16, 2048),
+        ]
         for i in range(2):
-            gather_x(i, span(0), xg_first[:, i, :])
-            gather_x(i, span(1, last), xg[:, i, :])
-        interleave(xb[last][:, :, 0:2], xg[:, 0:2, span(last - 1)])
-        for i in range(2, PACK):
-            gather_x(i, span(0), xg_first[:, i, :])
-            gather_x(i, span(1, 2), xg[:, i, span(0, 2)])
+            gather_x(i, span(0, CHUNKS), xg[:, i, :])
+        interleave(xb[0][:, :, 0:2], xg[:, 0:2, span(0)])
+        gather_x(2, span(0), xg_first[:, 0, :])
+        gather_x(2, span(1, last), xg[:, 2, span(1, last)])
+        interleave(xb[last][:, :, 0:3], xg[:, 0:3, span(last)])
+        gather_x(3, span(0), xg_first[:, 1, :])
+        gather_x(3, span(1), xg[:, 3, span(1)])
+        gather_x(3, span(2), xg[:, 3, span(2)])
 
         def quantize_x(c):
             quantize(x_codes[c], x_scales[c], xb[c])
@@ -245,33 +259,32 @@ def tile_list_htabg_mul_res_kernel(
             nc.gpsimd.tensor_tensor(sums[:], y_sb[:], residual(c, h), ADD)
             nc.sync.dma_start(out_rows[:, 2 * h : 2 * h + 2, span(c)], sums[:])
 
-        interleave(xb[0][:], xg_first[:])
+        interleave(xb[0][:, :, 2:PACK], xg_first[:])
         quantize_x(0)
-        xg_late = sb("xg_late", [P, 2, CHUNK], F32, on="xg_first")
-        for i in range(2):
-            gather_x(2 + i, span(last), xg_late[:, i, :])
-        interleave(xb[1][:], xg[:, :, span(0)])
-        quantize_x(1)
-        interleave(xb[2][:], xg[:, :, span(1)])
-        interleave(xb[last][:, :, 2:PACK], xg_late[:])
-        wd_b = [sb("wd_b%d" % h, [P, N // 2, PACK], BF16, on="xb%d" % h) for h in range(2)]
+        xg_late = sb("xg_late", [P, 1, CHUNK], F32, on="xg_first")
+        gather_x(3, span(last), xg_late[:, 0, :])
+        interleave(xb[1][:], xg[:, :, span(1)])
+        interleave(xb[2][:], xg[:, :, span(2)])
+        interleave(xb[last][:, :, 3:PACK], xg_late[:])
+        wd_b = [placed("wd_b0", [P, N // 2, PACK], BF16, 0), sb("wd_b1", [P, N // 2, PACK], BF16, on="xb1")]
         for h in range(2):
             interleave(wd_b[h][:], wd_raw[:, :, h * N // 2 : (h + 1) * N // 2])
+        quantize_x(1)
         product(0, 0)
         product(0, 1)
         quantize_x(2)
         quantize_h(0)
         quantize_x(3)
         product(1, 0)
-        quantize_wd(0)
         product(1, 1)
-        quantize_wd(1)
+        quantize_wd(0)
         quantize_h(1)
-        finish_on_gpsimd(0, 0, "hb1")
+        product(2, 0)
+        quantize_wd(1)
+        finish_on_gpsimd(0, 0, "xb1")
         yb.append(sb("yb3", [P, 2, CHUNK, 2], F32, on="wd_raw"))
         for u in range(2):
             copy_yb(last, u, held[u])
-        product(2, 0)
         product(2, 1)
         finish(1, 0)
         finish(1, 1)

@@ -70,7 +70,7 @@ def tile_list_htabg_mul_res_kernel(
         v_s = sb("v_s", [P, 2, J // 4], I32)
         yb = [sb("yb%d" % c, [P, 2, CHUNK, 2], F32) for c in range(CHUNKS - 1)]
         xg_first = sb("xg_first", [P, 2, CHUNK], F32)
-        xg = sb("xg", [P, PACK, J], F32)
+        xg = sb("xg", [P, 6, J], F32)
         x_codes = [sb("x_codes%d" % c, [P, CHUNK], U32) for c in range(CHUNKS)]
         x_scales = [sb("x_scales%d" % c, [P, CHUNK], U8) for c in range(CHUNKS)]
         wd_codes = [sb("wd_codes%d" % h, [P, N // 2], U32) for h in range(2)]
@@ -83,9 +83,9 @@ def tile_list_htabg_mul_res_kernel(
         nc.vector.memset(tab_s[32:64, :], 0)
         nc.vector.memset(tab_s[64:P, :], 0)
         nc.vector.memset(wgt_rows[64:P, :], 0.0)
+        nc.vector.memset(v_s[:], 0)
+        nc.vector.memset(wa_s_raw[:], 0)
         make_identity(nc, identity[:])
-        nc.gpsimd.memset(v_s[:], 0)
-        nc.gpsimd.memset(wa_s_raw[:], 0)
 
         x_rows = xT.rearrange("(p i) t -> i p t", i=PACK)
         wd_rows = wd.rearrange("(g t q) n -> t g q n", t=PACK, q=8)
@@ -194,12 +194,13 @@ def tile_list_htabg_mul_res_kernel(
         for i in range(2):
             gather_x(i, span(0, CHUNKS), xg[:, i, :])
         interleave(xb[0][:, :, 0:2], xg[:, 0:2, span(0)])
-        gather_x(2, span(0), xg_first[:, 0, :])
-        gather_x(2, span(1, last), xg[:, 2, span(1, last)])
+        gather_x(2, span(last), xg[:, 2, span(last)])
         interleave(xb[last][:, :, 0:3], xg[:, 0:3, span(last)])
+        gather_x(2, span(0), xg_first[:, 0, :])
+        gather_x(2, span(1, 2), xg[:, 3, span(1, 2)])
         gather_x(3, span(0), xg_first[:, 1, :])
-        gather_x(3, span(1), xg[:, 3, span(1)])
-        gather_x(3, span(2), xg[:, 3, span(2)])
+        gather_x(3, span(1), xg[:, 4, span(1)])
+        gather_x(3, span(2), xg[:, 4, span(2)])
 
         def quantize_x(c):
             quantize(x_codes[c], x_scales[c], xb[c])
@@ -263,8 +264,11 @@ def tile_list_htabg_mul_res_kernel(
         quantize_x(0)
         xg_late = sb("xg_late", [P, 1, CHUNK], F32, on="xg_first")
         gather_x(3, span(last), xg_late[:, 0, :])
-        interleave(xb[1][:], xg[:, :, span(1)])
-        interleave(xb[2][:], xg[:, :, span(2)])
+        for c in (1, 2):
+            planes = xg[:].rearrange("p (u r) j -> p u r j", u=2)[:, :, 0:2, span(c)]
+            nc.scalar.copy(
+                xb[c][:].rearrange("p (c e) (u v) -> p c u v e", e=4, v=2), planes.rearrange("p u v (c e) -> p c u v e", e=4)
+            )
         interleave(xb[last][:, :, 3:PACK], xg_late[:])
         wd_b = [placed("wd_b0", [P, N // 2, PACK], BF16, 0), sb("wd_b1", [P, N // 2, PACK], BF16, on="xb1")]
         for h in range(2):

@@ -22,6 +22,7 @@ PACK = 4
 GROUP = 128
 CHUNK = 256
 CHUNKS = J // CHUNK
+EARLY_BANKS = 2
 
 
 def tile_list_htabg_mul_res_kernel(
@@ -66,8 +67,8 @@ def tile_list_htabg_mul_res_kernel(
             placed("v_w2", [P, 2, 2 * CHUNK], U8, 1536) if c == 2 else sb("v_w%d" % c, [P, 2, 2 * CHUNK], U8)
             for c in range(CHUNKS)
         ]
-        v_rows = sb("v_rows", [P, J], U8)
-        v_s = sb("v_s", [P, 2, J // 4], I32)
+        v_s0 = sb("v_s0", [P, J], U8)
+        v_s1 = sb("v_s1", [P, J // 4], I32)
         yb = [sb("yb%d" % c, [P, 2, CHUNK, 2], F32) for c in range(CHUNKS - 1)]
         xg_first = sb("xg_first", [P, 2, CHUNK], F32)
         xg = sb("xg", [P, 6, J], F32)
@@ -79,11 +80,10 @@ def tile_list_htabg_mul_res_kernel(
         h_codes = [sb("h_codes%d" % c, [P, CHUNK], U32) for c in range(CHUNKS)]
         h_scales = [sb("h_scales%d" % c, [P, CHUNK], U8) for c in range(CHUNKS)]
 
-        nc.vector.memset(wb_s_raw[:], 0)
-        nc.vector.memset(tab_s[32:64, :], 0)
-        nc.vector.memset(tab_s[64:P, :], 0)
+        nc.vector.memset(tab_s[:], 0)
         nc.vector.memset(wgt_rows[64:P, :], 0.0)
-        nc.vector.memset(v_s[:], 0)
+        nc.vector.memset(wb_s_raw[:], 0)
+        nc.vector.memset(v_s1[:], 0)
         nc.vector.memset(wa_s_raw[:], 0)
         make_identity(nc, identity[:])
 
@@ -92,24 +92,23 @@ def tile_list_htabg_mul_res_kernel(
         res_rows = res.rearrange("(b p) j -> p b j", p=P)
         out_rows = out.rearrange("(b p) j -> p b j", p=P)
         word_rows = tab_words[0].rearrange("p t b -> p (t b)").bitcast(I32)
-        tab_rows = tab_scales.rearrange("a m t -> m a t")
+        tab_rows = tab_scales.rearrange("a (q s) t -> s q a t", s=4)
 
-        nc.sync.dma_start(tab_s[0:32, :], tab_rows.bitcast(I32))
-        nc.scalar.dma_start(wgt_rows[0:64, :], wgt2.rearrange("(g s) (b c) -> s b g c", s=16, c=P)[0])
         nc.sync.dma_start(idx[:], offs)
+        nc.sync.dma_start(wgt_rows[0:64, :], wgt2.rearrange("(g s) (b c) -> s b g c", s=16, c=P)[0])
+        for s in range(4):
+            nc.sync.dma_start(tab_s[s:P:16, :], tab_rows[s].bitcast(I32))
         nc.sync.dma_start(tab_w[:], word_rows)
         nc.sync.dma_start(wb_w_raw[:], wb_words.rearrange("a p c -> p a c").bitcast(I32))
         for q in range(4):
             nc.sync.dma_start(
                 wb_s_raw[32 * q : 32 * q + 4], wb_scales[:, 4 * q : 4 * q + 4, :].rearrange("a q c -> q a c").bitcast(I32)
             )
-        nc.sync.dma_start(x_planes[0][:], x_rows[0])
-        nc.vector.tensor_copy(v_rows[:], tab_s[:].bitcast(U8).indirect(idx[:]))
-        for q in range(4):
-            nc.sync.dma_start(
-                v_s[32 * q : 32 * q + 4].rearrange("p a c -> p (a c)"), v_rows[8 * q : 8 * q + 8, :].bitcast(I32)
-            )
         nc.sync.dma_start(idx2[:], offs2)
+        nc.sync.dma_start(x_planes[0][:], x_rows[0])
+        nc.vector.tensor_copy(v_s0[:], tab_s[:].bitcast(U8).indirect(idx[:]))
+        for q in range(0, P, 32):
+            nc.sync.dma_start(v_s1[q : q + 4, :], v_s0[q + 16 : q + 20, :].bitcast(I32))
         nc.sync.dma_start(x_planes[1][:], x_rows[1])
         nc.sync.dma_start(wa_w_raw[:], wa_words[0].bitcast(I32))
         for q in range(4):
@@ -124,7 +123,7 @@ def tile_list_htabg_mul_res_kernel(
         for c in range(CHUNKS):
             nc.vector.tensor_copy(v_pairs[:, span(c)], tab_w[:].bitcast(U32).indirect(idx[:, entries(span(c))]))
             nc.vector.tensor_copy(v_w[c][:].bitcast(U16), v_pairs[:, span(c)].bitcast(U16).rearrange("p (j a) -> p a j", a=2))
-        v_scales = [v_s[:, a, :].bitcast(U8) for a in range(2)]
+        v_scales = (v_s0[:], v_s1[:].bitcast(U8))
 
         turned = psum_late.tile([P, P], F32, name="second")
         nc.tensor.transpose(turned[:], wgt_rows[:], identity[:])
@@ -156,7 +155,8 @@ def tile_list_htabg_mul_res_kernel(
         for c in range(CHUNKS):
             for u in range(2):
                 bank = (psum if c < last else psum_late).tile([P, 2, CHUNK], F32, name="first" if c < last else "second")
-                for a in range(2):
+                order = (0, 1) if 2 * c + u < EARLY_BANKS else (1, 0)
+                for a in order:
                     for e in range(2):
                         nc.tensor.matmul_mx(
                             out=bank[:, e, :],
@@ -164,8 +164,8 @@ def tile_list_htabg_mul_res_kernel(
                             lhsT_scale=wb_s[:, 2 * u + e, a, :].bitcast(U8),
                             rhs=v_w[c][:, a, :].bitcast(FP4X4),
                             rhs_scale=v_scales[a][:, span(c)],
-                            start=(a == 0 and e == 0),
-                            stop=(a == 1 and e == 1),
+                            start=(a == order[0] and e == 0),
+                            stop=(a == order[1] and e == 1),
                         )
                 if c < last:
                     copy_yb(c, u, bank)
@@ -187,7 +187,7 @@ def tile_list_htabg_mul_res_kernel(
 
         xb = [
             placed("xb0", [P, CHUNK, PACK], BF16, 0),
-            sb("xb1", [P, CHUNK, PACK], BF16),
+            placed("xb1", [P, CHUNK, PACK], BF16, 5120),
             sb("xb2", [P, CHUNK, PACK], BF16),
             placed("xb3", [P, CHUNK, PACK], BF16, 2048),
         ]
@@ -253,10 +253,9 @@ def tile_list_htabg_mul_res_kernel(
             nc.vector.tensor_tensor(sums[:], second(c, h)[:], residual(c, h), ADD)
             nc.sync.dma_start(out_rows[:, 2 * h : 2 * h + 2, span(c)], sums[:])
 
-        def finish_on_gpsimd(c, h, on):
+        def finish_on_gpsimd(c, h, sums):
             y_sb = sb("y_sb%d%d" % (c, h), [P, 2, CHUNK], F32)
             nc.scalar.copy(y_sb[:], second(c, h)[:])
-            sums = sb("sums%d%d" % (c, h), [P, 2, CHUNK], F32, on=on)
             nc.gpsimd.tensor_tensor(sums[:], y_sb[:], residual(c, h), ADD)
             nc.sync.dma_start(out_rows[:, 2 * h : 2 * h + 2, span(c)], sums[:])
 
@@ -270,7 +269,7 @@ def tile_list_htabg_mul_res_kernel(
                 xb[c][:].rearrange("p (c e) (u v) -> p c u v e", e=4, v=2), planes.rearrange("p u v (c e) -> p c u v e", e=4)
             )
         interleave(xb[last][:, :, 3:PACK], xg_late[:])
-        wd_b = [placed("wd_b0", [P, N // 2, PACK], BF16, 0), sb("wd_b1", [P, N // 2, PACK], BF16, on="xb1")]
+        wd_b = [placed("wd_b0", [P, N // 2, PACK], BF16, 0), placed("wd_b1", [P, N // 2, PACK], BF16, 5120)]
         for h in range(2):
             interleave(wd_b[h][:], wd_raw[:, :, h * N // 2 : (h + 1) * N // 2])
         quantize_x(1)
@@ -285,15 +284,15 @@ def tile_list_htabg_mul_res_kernel(
         quantize_h(1)
         product(2, 0)
         quantize_wd(1)
-        finish_on_gpsimd(0, 0, "xb1")
-        yb.append(sb("yb3", [P, 2, CHUNK, 2], F32, on="wd_raw"))
+        finish_on_gpsimd(0, 0, placed("sums00", [P, 2, CHUNK], F32, 4096))
+        yb.append(placed("yb3", [P, 2, CHUNK, 2], F32, 6144))
         for u in range(2):
             copy_yb(last, u, held[u])
         product(2, 1)
         finish(1, 0)
         finish(1, 1)
         quantize_h(2)
-        finish_on_gpsimd(0, 1, "hb2")
+        finish_on_gpsimd(0, 1, sb("sums01", [P, 2, CHUNK], F32, on="hb2"))
         product(3, 0)
         product(3, 1)
         finish(2, 0)

@@ -69,7 +69,7 @@ def tile_list_htabg_mul_res_kernel(
         ]
         v_s0 = sb("v_s0", [P, J], U8)
         v_s1 = sb("v_s1", [P, J // 4], I32)
-        yb = [sb("yb%d" % c, [P, 2, CHUNK, 2], F32) for c in range(CHUNKS - 1)]
+        yb = [sb("yb%d" % c, [P, PACK, CHUNK], F32) for c in range(CHUNKS - 1)]
         xg_first = sb("xg_first", [P, 2, CHUNK], F32)
         xg = sb("xg", [P, 6, J], F32)
         x_codes = [sb("x_codes%d" % c, [P, CHUNK], U32) for c in range(CHUNKS)]
@@ -150,7 +150,7 @@ def tile_list_htabg_mul_res_kernel(
         held = []
 
         def copy_yb(c, u, bank):
-            nc.scalar.copy(yb[c][:, u], bank[:].rearrange("p e j -> p j e"))
+            nc.scalar.copy(yb[c][:, 2 * u : 2 * u + 2, :], bank[:])
 
         for c in range(CHUNKS):
             for u in range(2):
@@ -225,9 +225,9 @@ def tile_list_htabg_mul_res_kernel(
                     stop=True,
                 )
             nc.vector.tensor_tensor(
-                hb[c][:, within, :].rearrange("p j (u e) -> p j u e", e=2),
-                bank[:].rearrange("p (u e) j -> p j u e", e=2),
-                yb[c][:, :, within, :].rearrange("p u j e -> p j u e"),
+                hb[c][:, within, :].rearrange("p (j e) t -> p j t e", e=2),
+                bank[:].rearrange("p t (j e) -> p j t e", e=2),
+                yb[c][:, :, within].rearrange("p t (j e) -> p j t e", e=2),
                 MULT,
             )
 
@@ -285,7 +285,7 @@ def tile_list_htabg_mul_res_kernel(
         product(2, 0)
         quantize_wd(1)
         finish_on_gpsimd(0, 0, placed("sums00", [P, 2, CHUNK], F32, 4096))
-        yb.append(placed("yb3", [P, 2, CHUNK, 2], F32, 6144))
+        yb.append(placed("yb3", [P, PACK, CHUNK], F32, 6144))
         for u in range(2):
             copy_yb(last, u, held[u])
         product(2, 1)

@@ -22,7 +22,6 @@ PACK = 4
 GROUP = 128
 CHUNK = 256
 CHUNKS = J // CHUNK
-EARLY_BANKS = 2
 
 
 def tile_list_htabg_mul_res_kernel(
@@ -56,7 +55,7 @@ def tile_list_htabg_mul_res_kernel(
         wgt_wide = sb("wgt_wide", [P, J], F32)
         identity = sb("identity", [P, P], F32)
         x_planes = [sb("x_plane%d" % i, [P, T], F32) for i in range(PACK)]
-        wa_w_raw = sb("wa_w_raw", [P, 256], I32)
+        wa_w_raw = placed("wa_w_raw", [P, 256], I32, 9152)
         wa_s_raw = sb("wa_s_raw", [P, 128], I32)
         wb_w_raw = sb("wb_w_raw", [P, 2, 256], I32)
         wb_s_raw = sb("wb_s_raw", [P, 2, 128], I32)
@@ -67,10 +66,10 @@ def tile_list_htabg_mul_res_kernel(
             placed("v_w2", [P, 2, 2 * CHUNK], U8, 1536) if c == 2 else sb("v_w%d" % c, [P, 2, 2 * CHUNK], U8)
             for c in range(CHUNKS)
         ]
-        v_s0 = sb("v_s0", [P, J], U8)
-        v_s1 = sb("v_s1", [P, J // 4], I32)
+        v_rows = sb("v_rows", [P, J], U8)
+        v_s = sb("v_s", [P, 2, J // 4], I32)
         yb = [sb("yb%d" % c, [P, PACK, CHUNK], F32) for c in range(CHUNKS - 1)]
-        xg_first = sb("xg_first", [P, 2, CHUNK], F32)
+        xg_first = placed("xg_first", [P, 2, CHUNK], F32, 10240)
         xg = sb("xg", [P, 6, J], F32)
         x_codes = [sb("x_codes%d" % c, [P, CHUNK], U32) for c in range(CHUNKS)]
         x_scales = [sb("x_scales%d" % c, [P, CHUNK], U8) for c in range(CHUNKS)]
@@ -80,11 +79,12 @@ def tile_list_htabg_mul_res_kernel(
         h_codes = [sb("h_codes%d" % c, [P, CHUNK], U32) for c in range(CHUNKS)]
         h_scales = [sb("h_scales%d" % c, [P, CHUNK], U8) for c in range(CHUNKS)]
 
-        nc.vector.memset(tab_s[:], 0)
+        nc.vector.memset(tab_s[0:64], 0)
+        nc.vector.memset(tab_s[96:P], 0)
         nc.vector.memset(wgt_rows[64:P, :], 0.0)
         nc.vector.memset(wb_s_raw[:], 0)
-        nc.vector.memset(v_s1[:], 0)
-        nc.vector.memset(wa_s_raw[:], 0)
+        nc.gpsimd.memset(v_s[:], 0)
+        nc.gpsimd.memset(wa_s_raw[:], 0)
         make_identity(nc, identity[:])
 
         x_rows = xT.rearrange("(p i) t -> i p t", i=PACK)
@@ -92,12 +92,11 @@ def tile_list_htabg_mul_res_kernel(
         res_rows = res.rearrange("(b p) j -> p b j", p=P)
         out_rows = out.rearrange("(b p) j -> p b j", p=P)
         word_rows = tab_words[0].rearrange("p t b -> p (t b)").bitcast(I32)
-        tab_rows = tab_scales.rearrange("a (q s) t -> s q a t", s=4)
+        tab_rows = tab_scales.rearrange("a q t -> q a t")
 
+        nc.sync.dma_start(tab_s[64:96, :], tab_rows.bitcast(I32))
         nc.sync.dma_start(idx[:], offs)
         nc.sync.dma_start(wgt_rows[0:64, :], wgt2.rearrange("(g s) (b c) -> s b g c", s=16, c=P)[0])
-        for s in range(4):
-            nc.sync.dma_start(tab_s[s:P:16, :], tab_rows[s].bitcast(I32))
         nc.sync.dma_start(tab_w[:], word_rows)
         nc.sync.dma_start(wb_w_raw[:], wb_words.rearrange("a p c -> p a c").bitcast(I32))
         for q in range(4):
@@ -106,15 +105,14 @@ def tile_list_htabg_mul_res_kernel(
             )
         nc.sync.dma_start(idx2[:], offs2)
         nc.sync.dma_start(x_planes[0][:], x_rows[0])
-        nc.vector.tensor_copy(v_s0[:], tab_s[:].bitcast(U8).indirect(idx[:]))
-        for q in range(0, P, 32):
-            nc.sync.dma_start(v_s1[q : q + 4, :], v_s0[q + 16 : q + 20, :].bitcast(I32))
-        nc.sync.dma_start(x_planes[1][:], x_rows[1])
-        nc.sync.dma_start(wa_w_raw[:], wa_words[0].bitcast(I32))
+        nc.vector.tensor_copy(v_rows[:], tab_s[:].bitcast(U8).indirect(idx[:]))
+        for q in range(4):
+            nc.sync.dma_start(v_s[32 * q : 32 * q + 4], v_rows[64 + 8 * q : 72 + 8 * q, :].bitcast(I32))
+        for i in range(1, PACK):
+            nc.sync.dma_start(x_planes[i][:], x_rows[i])
         for q in range(4):
             nc.sync.dma_start(wa_s_raw[32 * q : 32 * q + 4, :], wa_scales[0, 4 * q : 4 * q + 4, :].bitcast(I32))
-        nc.sync.dma_start(x_planes[2][:], x_rows[2])
-        nc.sync.dma_start(x_planes[3][:], x_rows[3])
+        nc.sync.dma_start(wa_w_raw[:], wa_words[0].bitcast(I32))
         for t in range(PACK):
             nc.sync.dma_start(wd_raw[:, t, :], wd_rows[t])
         for h in range(2):
@@ -123,7 +121,6 @@ def tile_list_htabg_mul_res_kernel(
         for c in range(CHUNKS):
             nc.vector.tensor_copy(v_pairs[:, span(c)], tab_w[:].bitcast(U32).indirect(idx[:, entries(span(c))]))
             nc.vector.tensor_copy(v_w[c][:].bitcast(U16), v_pairs[:, span(c)].bitcast(U16).rearrange("p (j a) -> p a j", a=2))
-        v_scales = (v_s0[:], v_s1[:].bitcast(U8))
 
         turned = psum_late.tile([P, P], F32, name="second")
         nc.tensor.transpose(turned[:], wgt_rows[:], identity[:])
@@ -155,26 +152,21 @@ def tile_list_htabg_mul_res_kernel(
         for c in range(CHUNKS):
             for u in range(2):
                 bank = (psum if c < last else psum_late).tile([P, 2, CHUNK], F32, name="first" if c < last else "second")
-                order = (0, 1) if 2 * c + u < EARLY_BANKS else (1, 0)
-                for a in order:
+                for a in range(2):
                     for e in range(2):
                         nc.tensor.matmul_mx(
                             out=bank[:, e, :],
                             lhsT=wb_w[:, 2 * u + e, a, :].bitcast(FP4X4),
                             lhsT_scale=wb_s[:, 2 * u + e, a, :].bitcast(U8),
                             rhs=v_w[c][:, a, :].bitcast(FP4X4),
-                            rhs_scale=v_scales[a][:, span(c)],
-                            start=(a == order[0] and e == 0),
-                            stop=(a == order[1] and e == 1),
+                            rhs_scale=v_s[:, a, :].bitcast(U8)[:, span(c)],
+                            start=(a == 0 and e == 0),
+                            stop=(a == 1 and e == 1),
                         )
                 if c < last:
                     copy_yb(c, u, bank)
                 else:
                     held.append(bank)
-        wa_w = sb("wa_w", [P, PACK, 64], I32, on="wgt_wide")
-        wa_s = sb("wa_s", [P, PACK, 32], I32, on="identity")
-        regroup(wa_w[:], wa_w_raw[:], 4)
-        regroup(wa_s[:], wa_s_raw[:], 2)
 
         def interleave(packed, planes):
             nc.scalar.copy(packed.rearrange("p (c e) t -> p c t e", e=4), planes.rearrange("p t (c e) -> p c t e", e=4))
@@ -185,10 +177,11 @@ def tile_list_htabg_mul_res_kernel(
         def quantize(codes, scales, values):
             nc.vector.quantize_mx(out=codes[:].bitcast(FP8X4), scales=scales[:], in_=values[:].rearrange("p j t -> p (j t)"))
 
+        xb_middle = placed("xb_middle", [P, 2 * CHUNK, PACK], BF16, 5120)
         xb = [
             placed("xb0", [P, CHUNK, PACK], BF16, 0),
-            placed("xb1", [P, CHUNK, PACK], BF16, 5120),
-            sb("xb2", [P, CHUNK, PACK], BF16),
+            xb_middle[:, span(0), :],
+            xb_middle[:, span(1), :],
             placed("xb3", [P, CHUNK, PACK], BF16, 2048),
         ]
         for i in range(2):
@@ -260,8 +253,12 @@ def tile_list_htabg_mul_res_kernel(
             nc.sync.dma_start(out_rows[:, 2 * h : 2 * h + 2, span(c)], sums[:])
 
         interleave(xb[0][:, :, 2:PACK], xg_first[:])
+        wa_w = sb("wa_w", [P, PACK, 64], I32, on="wgt_wide")
+        wa_s = sb("wa_s", [P, PACK, 32], I32, on="identity")
+        regroup(wa_s[:], wa_s_raw[:], 2)
+        regroup(wa_w[:], wa_w_raw[:], 4)
         quantize_x(0)
-        xg_late = sb("xg_late", [P, 1, CHUNK], F32, on="xg_first")
+        xg_late = placed("xg_late", [P, 1, CHUNK], F32, 9728)
         gather_x(3, span(last), xg_late[:, 0, :])
         for c in (1, 2):
             planes = xg[:].rearrange("p (u r) j -> p u r j", u=2)[:, :, 0:2, span(c)]
@@ -269,7 +266,7 @@ def tile_list_htabg_mul_res_kernel(
                 xb[c][:].rearrange("p (c e) (u v) -> p c u v e", e=4, v=2), planes.rearrange("p u v (c e) -> p c u v e", e=4)
             )
         interleave(xb[last][:, :, 3:PACK], xg_late[:])
-        wd_b = [placed("wd_b0", [P, N // 2, PACK], BF16, 0), placed("wd_b1", [P, N // 2, PACK], BF16, 5120)]
+        wd_b = [placed("wd_b0", [P, N // 2, PACK], BF16, 10240), placed("wd_b1", [P, N // 2, PACK], BF16, 5120)]
         for h in range(2):
             interleave(wd_b[h][:], wd_raw[:, :, h * N // 2 : (h + 1) * N // 2])
         quantize_x(1)

@@ -83,8 +83,8 @@ def tile_list_htabg_mul_res_kernel(
         nc.vector.memset(tab_s[96:P], 0)
         nc.vector.memset(wgt_rows[64:P, :], 0.0)
         nc.vector.memset(wb_s_raw[:], 0)
-        nc.gpsimd.memset(v_s[:], 0)
-        nc.gpsimd.memset(wa_s_raw[:], 0)
+        nc.vector.memset(v_s[:], 0)
+        nc.vector.memset(wa_s_raw[:], 0)
         make_identity(nc, identity[:])
 
         x_rows = xT.rearrange("(p i) t -> i p t", i=PACK)
@@ -151,7 +151,8 @@ def tile_list_htabg_mul_res_kernel(
 
         for c in range(CHUNKS):
             for u in range(2):
-                bank = (psum if c < last else psum_late).tile([P, 2, CHUNK], F32, name="first" if c < last else "second")
+                early = 2 * c + u < 3
+                bank = (psum if early else psum_late).tile([P, 2, CHUNK], F32, name="first" if early else "second")
                 for a in range(2):
                     for e in range(2):
                         nc.tensor.matmul_mx(

@@ -86,6 +86,10 @@ def tile_list_htabg_mul_res_kernel(
         nc.vector.memset(v_s[:], 0)
         nc.vector.memset(wa_s_raw[:], 0)
         make_identity(nc, identity[:])
+        warm = sb("warm", [P, 2, 2, 16], F32)
+        nc.gpsimd.memset(warm[:], 1.0)
+        warm_sum = sb("warm_sum", [P, 2, 16], F32)
+        nc.gpsimd.tensor_tensor(warm_sum[:], warm[:, 0], warm[:, :, 1], ADD)
 
         x_rows = xT.rearrange("(p i) t -> i p t", i=PACK)
         wd_rows = wd.rearrange("(g t q) n -> t g q n", t=PACK, q=8)

from contextlib import ExitStack

import concourse.mybir as mybir
from concourse.masks import make_identity

K, L, R, N, T, J = 512, 1024, 512, 512, 2048, 1024
FLOPS = 2 * J * R * (K + L + N)

F32 = mybir.dt.float32
BF16 = mybir.dt.bfloat16
I32 = mybir.dt.int32
U32 = mybir.dt.uint32
U16 = mybir.dt.uint16
U8 = mybir.dt.uint8
FP8X4 = mybir.dt.float8_e4m3fn_x4
FP4X4 = mybir.dt.float4_e2m1fn_x4
MULT = mybir.AluOpType.mult
ADD = mybir.AluOpType.add

P = 128
PACK = 4
GROUP = 128
CHUNK = 256
CHUNKS = J // CHUNK


def tile_list_htabg_mul_res_kernel(
    tc, tab_words, tab_scales, xT, wgt2, wa_words, wa_scales, wb_words, wb_scales, wd, res, offs, offs2, out
):
    nc = tc.nc
    with ExitStack() as ctx:
        keep = ctx.enter_context(tc.tile_pool(name="keep", bufs=1))
        shared = ctx.enter_context(tc.tile_pool(name="shared", bufs=1))
        psum = ctx.enter_context(tc.psum_pool(name="psum", bufs=3))
        psum_late = ctx.enter_context(tc.psum_pool(name="psum_late", bufs=5))

        def sb(name, shape, dtype, on=""):
            return keep.tile(shape, dtype, name=name, tag=on or name, align_bytes=64)

        def placed(name, shape, dtype, offset):
            return shared.tile(shape, dtype, name=name, align_bytes=64, offset=offset)

        def span(c, count=1):
            return slice(c * CHUNK, (c + count) * CHUNK)

        def entries(cols):
            return slice(cols.start // 16, cols.stop // 16)

        idx = sb("idx", [P, J // 16], U16)
        idx2 = sb("idx2", [P, J // 16], U16)
        tab_w = sb("tab_w", [P, T], I32)
        tab_s = sb("tab_s", [P, T // 4], I32)
        wgt = sb("wgt", [P, J], F32)
        wgt_rows = sb("wgt_rows", [P, P], F32)
        wgt_wide = sb("wgt_wide", [P, J], F32)
        identity = sb("identity", [P, P], F32)
        x_planes = [sb("x_plane%d" % i, [P, T], F32) for i in range(PACK)]
        wa_w_raw = placed("wa_w_raw", [P, 256], I32, 9152)
        wa_s_raw = sb("wa_s_raw", [P, 128], I32)
        wb_w_raw = sb("wb_w_raw", [P, 2, 256], I32)
        wb_s_raw = sb("wb_s_raw", [P, 2, 128], I32)
        wd_raw = sb("wd_raw", [P, PACK, N], F32)
        res_sb = [sb("res%d" % h, [P, N // P, J // 2], F32) for h in range(2)]
        v_pairs = sb("v_pairs", [P, J], U32)
        v_w = [
            placed("v_w2", [P, 2, 2 * CHUNK], U8, 1536) if c == 2 else sb("v_w%d" % c, [P, 2, 2 * CHUNK], U8)
            for c in range(CHUNKS)
        ]
        v_rows = sb("v_rows", [P, J], U8)
        v_s = sb("v_s", [P, 2, J // 4], I32)
        yb = [sb("yb%d" % c, [P, PACK, CHUNK], F32) for c in range(CHUNKS - 1)]
        xg_first = placed("xg_first", [P, 2, CHUNK], F32, 10240)
        xg = sb("xg", [P, 6, J], F32)
        x_codes = [sb("x_codes%d" % c, [P, CHUNK], U32) for c in range(CHUNKS)]
        x_scales = [sb("x_scales%d" % c, [P, CHUNK], U8) for c in range(CHUNKS)]
        wd_codes = [sb("wd_codes%d" % h, [P, N // 2], U32) for h in range(2)]
        wd_scales = [sb("wd_scales%d" % h, [P, N // 2], U8) for h in range(2)]
        hb = [sb("hb%d" % c, [P, CHUNK, PACK], BF16) for c in range(CHUNKS)]
        h_codes = [sb("h_codes%d" % c, [P, CHUNK], U32) for c in range(CHUNKS)]
        h_scales = [sb("h_scales%d" % c, [P, CHUNK], U8) for c in range(CHUNKS)]

        nc.vector.memset(tab_s[0:64], 0)
        nc.vector.memset(tab_s[96:P], 0)
        nc.vector.memset(wgt_rows[64:P, :], 0.0)
        nc.vector.memset(wb_s_raw[:], 0)
        nc.vector.memset(v_s[:], 0)
        nc.vector.memset(wa_s_raw[:], 0)
        make_identity(nc, identity[:])
        warm = sb("warm", [P, 2, 2, 16], F32)
        nc.gpsimd.memset(warm[:], 1.0)
        warm_sum = sb("warm_sum", [P, 2, 16], F32)
        nc.gpsimd.tensor_tensor(warm_sum[:], warm[:, 0], warm[:, :, 1], ADD)

        x_rows = xT.rearrange("(p i) t -> i p t", i=PACK)
        wd_rows = wd.rearrange("(g t q) n -> t g q n", t=PACK, q=8)
        res_rows = res.rearrange("(b p) j -> p b j", p=P)
        out_rows = out.rearrange("(b p) j -> p b j", p=P)
        word_rows = tab_words[0].rearrange("p t b -> p (t b)").bitcast(I32)
        tab_rows = tab_scales.rearrange("a q t -> q a t")

        nc.sync.dma_start(tab_s[64:96, :], tab_rows.bitcast(I32))
        nc.sync.dma_start(idx[:], offs)
        nc.sync.dma_start(wgt_rows[0:64, :], wgt2.rearrange("(g s) (b c) -> s b g c", s=16, c=P)[0])
        nc.sync.dma_start(tab_w[:], word_rows)
        nc.sync.dma_start(wb_w_raw[:], wb_words.rearrange("a p c -> p a c").bitcast(I32))
        for q in range(4):
            nc.sync.dma_start(
                wb_s_raw[32 * q : 32 * q + 4], wb_scales[:, 4 * q : 4 * q + 4, :].rearrange("a q c -> q a c").bitcast(I32)
            )
        nc.sync.dma_start(idx2[:], offs2)
        nc.sync.dma_start(x_planes[0][:], x_rows[0])
        nc.vector.tensor_copy(v_rows[:], tab_s[:].bitcast(U8).indirect(idx[:]))
        for q in range(4):
            nc.sync.dma_start(v_s[32 * q : 32 * q + 4], v_rows[64 + 8 * q : 72 + 8 * q, :].bitcast(I32))
        for i in range(1, PACK):
            nc.sync.dma_start(x_planes[i][:], x_rows[i])
        for q in range(4):
            nc.sync.dma_start(wa_s_raw[32 * q : 32 * q + 4, :], wa_scales[0, 4 * q : 4 * q + 4, :].bitcast(I32))
        nc.sync.dma_start(wa_w_raw[:], wa_words[0].bitcast(I32))
        for t in range(PACK):
            nc.sync.dma_start(wd_raw[:, t, :], wd_rows[t])
        for h in range(2):
            nc.sync.dma_start(res_sb[h][:], res_rows[:, :, span(2 * h, 2)])

        for c in range(CHUNKS):
            nc.vector.tensor_copy(v_pairs[:, span(c)], tab_w[:].bitcast(U32).indirect(idx[:, entries(span(c))]))
            nc.vector.tensor_copy(v_w[c][:].bitcast(U16), v_pairs[:, span(c)].bitcast(U16).rearrange("p (j a) -> p a j", a=2))

        turned = psum_late.tile([P, P], F32, name="second")
        nc.tensor.transpose(turned[:], wgt_rows[:], identity[:])
        nc.scalar.copy(
            wgt_wide[:].rearrange("p (m s) -> p m s", s=16), turned[:, 0:64].unsqueeze(2).to_broadcast([P, 64, 16])
        )
        for c in range(CHUNKS):
            bank = psum.tile([P, CHUNK], F32, name="first")
            for b in range(0, CHUNK, P):
                nc.tensor.transpose(bank[:, b : b + P], wgt_wide[:, c * CHUNK + b : c * CHUNK + b + P], identity[:])
            nc.scalar.copy(wgt[:, span(c)], bank[:])

        def regroup(grouped, raw, e):
            nc.scalar.copy(
                grouped.bitcast(U32).rearrange("p t (g e) -> p t g e", e=e),
                raw.bitcast(U32).rearrange("p (g t e) -> p t g e", t=PACK, e=e),
            )

        wb_w = sb("wb_w", [P, PACK, 2, 64], I32, on="wgt_wide")
        wb_s = sb("wb_s", [P, PACK, 2, 32], I32, on="identity")
        regroup(wb_w[:].rearrange("p t a c -> p t (a c)"), wb_w_raw[:].rearrange("p a c -> p (a c)"), 4)
        regroup(wb_s[:].rearrange("p t a c -> p t (a c)"), wb_s_raw[:].rearrange("p a c -> p (a c)"), 2)
        last = CHUNKS - 1
        held = []

        def copy_yb(c, u, bank):
            nc.scalar.copy(yb[c][:, 2 * u : 2 * u + 2, :], bank[:])

        for c in range(CHUNKS):
            for u in range(2):
                early = 2 * c + u < 3
                bank = (psum if early else psum_late).tile([P, 2, CHUNK], F32, name="first" if early else "second")
                for a in range(2):
                    for e in range(2):
                        nc.tensor.matmul_mx(
                            out=bank[:, e, :],
                            lhsT=wb_w[:, 2 * u + e, a, :].bitcast(FP4X4),
                            lhsT_scale=wb_s[:, 2 * u + e, a, :].bitcast(U8),
                            rhs=v_w[c][:, a, :].bitcast(FP4X4),
                            rhs_scale=v_s[:, a, :].bitcast(U8)[:, span(c)],
                            start=(a == 0 and e == 0),
                            stop=(a == 1 and e == 1),
                        )
                if c < last:
                    copy_yb(c, u, bank)
                else:
                    held.append(bank)

        def interleave(packed, planes):
            nc.scalar.copy(packed.rearrange("p (c e) t -> p c t e", e=4), planes.rearrange("p t (c e) -> p c t e", e=4))

        def gather_x(i, cols, picked):
            nc.vector.tensor_tensor(picked, x_planes[i][:].indirect(idx2[:, entries(cols)]), wgt[:, cols], MULT)

        def quantize(codes, scales, values):
            nc.vector.quantize_mx(out=codes[:].bitcast(FP8X4), scales=scales[:], in_=values[:].rearrange("p j t -> p (j t)"))

        xb_middle = placed("xb_middle", [P, 2 * CHUNK, PACK], BF16, 5120)
        xb = [
            placed("xb0", [P, CHUNK, PACK], BF16, 0),
            xb_middle[:, span(0), :],
            xb_middle[:, span(1), :],
            placed("xb3", [P, CHUNK, PACK], BF16, 2048),
        ]
        for i in range(2):
            gather_x(i, span(0, CHUNKS), xg[:, i, :])
        interleave(xb[0][:, :, 0:2], xg[:, 0:2, span(0)])
        gather_x(2, span(last), xg[:, 2, span(last)])
        interleave(xb[last][:, :, 0:3], xg[:, 0:3, span(last)])
        gather_x(2, span(0), xg_first[:, 0, :])
        gather_x(2, span(1, 2), xg[:, 3, span(1, 2)])
        gather_x(3, span(0), xg_first[:, 1, :])
        gather_x(3, span(1), xg[:, 4, span(1)])
        gather_x(3, span(2), xg[:, 4, span(2)])

        def quantize_x(c):
            quantize(x_codes[c], x_scales[c], xb[c])

        def quantize_h(c):
            quantize(h_codes[c], h_scales[c], hb[c])

        def quantize_wd(h):
            quantize(wd_codes[h], wd_scales[h], wd_b[h])

        def product(c, g):
            within = slice(g * GROUP, (g + 1) * GROUP)
            bank = psum.tile([P, PACK, GROUP], F32, name="first")
            for t in range(PACK):
                nc.tensor.matmul_mx(
                    out=bank[:, t, :],
                    lhsT=wa_w[:, t, :].bitcast(FP4X4),
                    lhsT_scale=wa_s[:, t, :].bitcast(U8),
                    rhs=x_codes[c][:, within].bitcast(FP8X4),
                    rhs_scale=x_scales[c][:, within],
                    start=True,
                    stop=True,
                )
            nc.vector.tensor_tensor(
                hb[c][:, within, :].rearrange("p (j e) t -> p j t e", e=2),
                bank[:].rearrange("p t (j e) -> p j t e", e=2),
                yb[c][:, :, within].rearrange("p t (j e) -> p j t e", e=2),
                MULT,
            )

        def second(c, h):
            bank = psum_late.tile([P, 2, CHUNK], F32, name="second")
            for b in range(2):
                nc.tensor.matmul_mx(
                    out=bank[:, b, :],
                    lhsT=wd_codes[h][:, b * P : (b + 1) * P].bitcast(FP8X4),
                    lhsT_scale=wd_scales[h][:, b * P : (b + 1) * P],
                    rhs=h_codes[c][:].bitcast(FP8X4),
                    rhs_scale=h_scales[c][:],
                    start=True,
                    stop=True,
                )
            return bank

        def residual(c, h):
            return res_sb[c // 2][:, 2 * h : 2 * h + 2, span(c % 2)]

        def finish(c, h):
            sums = sb("sums%d%d" % (c, h), [P, 2, CHUNK], F32)
            nc.vector.tensor_tensor(sums[:], second(c, h)[:], residual(c, h), ADD)
            nc.sync.dma_start(out_rows[:, 2 * h : 2 * h + 2, span(c)], sums[:])

        def finish_on_gpsimd(c, h, sums):
            y_sb = sb("y_sb%d%d" % (c, h), [P, 2, CHUNK], F32)
            nc.scalar.copy(y_sb[:], second(c, h)[:])
            nc.gpsimd.tensor_tensor(sums[:], y_sb[:], residual(c, h), ADD)
            nc.sync.dma_start(out_rows[:, 2 * h : 2 * h + 2, span(c)], sums[:])

        interleave(xb[0][:, :, 2:PACK], xg_first[:])
        wa_w = sb("wa_w", [P, PACK, 64], I32, on="wgt_wide")
        wa_s = sb("wa_s", [P, PACK, 32], I32, on="identity")
        regroup(wa_s[:], wa_s_raw[:], 2)
        regroup(wa_w[:], wa_w_raw[:], 4)
        quantize_x(0)
        xg_late = placed("xg_late", [P, 1, CHUNK], F32, 9728)
        gather_x(3, span(last), xg_late[:, 0, :])
        for c in (1, 2):
            planes = xg[:].rearrange("p (u r) j -> p u r j", u=2)[:, :, 0:2, span(c)]
            nc.scalar.copy(
                xb[c][:].rearrange("p (c e) (u v) -> p c u v e", e=4, v=2), planes.rearrange("p u v (c e) -> p c u v e", e=4)
            )
        interleave(xb[last][:, :, 3:PACK], xg_late[:])
        wd_b = [placed("wd_b0", [P, N // 2, PACK], BF16, 10240), placed("wd_b1", [P, N // 2, PACK], BF16, 5120)]
        for h in range(2):
            interleave(wd_b[h][:], wd_raw[:, :, h * N // 2 : (h + 1) * N // 2])
        quantize_x(1)
        product(0, 0)
        product(0, 1)
        quantize_x(2)
        quantize_h(0)
        quantize_x(3)
        product(1, 0)
        product(1, 1)
        quantize_wd(0)
        quantize_h(1)
        product(2, 0)
        quantize_wd(1)
        finish_on_gpsimd(0, 0, placed("sums00", [P, 2, CHUNK], F32, 4096))
        yb.append(placed("yb3", [P, PACK, CHUNK], F32, 6144))
        for u in range(2):
            copy_yb(last, u, held[u])
        product(2, 1)
        finish(1, 0)
        finish(1, 1)
        quantize_h(2)
        finish_on_gpsimd(0, 1, sb("sums01", [P, 2, CHUNK], F32, on="hb2"))
        product(3, 0)
        product(3, 1)
        finish(2, 0)
        quantize_h(3)
        finish(2, 1)
        finish(3, 0)
        bank = second(last, 1)
        for b in range(2):
            sums = sb("sums_last%d" % b, [P, CHUNK], F32)
            nc.vector.tensor_tensor(sums[:], bank[:, b, :], residual(last, 1)[:, b, :], ADD)
            (nc.sync, nc.scalar)[b].dma_start(out_rows[:, 2 + b, span(last)], sums[:])
